import numpy as np
import ml_dtypes


def mxq(x, axis, fmt="e4m3"):
    dtype, down = {"e4m3": (ml_dtypes.float8_e4m3fn, 7), "e5m2": (ml_dtypes.float8_e5m2, 14)}[fmt]
    v = np.moveaxis(np.asarray(x, np.float32).astype(ml_dtypes.bfloat16).astype(np.float64), axis, -1)
    blocks = v.reshape(v.shape[:-1] + (-1, 32))
    amax = np.abs(blocks).max(-1, keepdims=True)
    byte = np.maximum(np.where(amax > 0, np.frexp(amax)[1] - 1 + 127, 0) - down, 1)
    scale = np.exp2(byte - 127.0)
    codes = (blocks / scale).astype(np.float32).astype(dtype).astype(np.float64)
    return np.moveaxis((codes * scale).reshape(v.shape), -1, axis)


WIDE = False


def mx_kscale(k):
    if not WIDE:
        return np.ones(k)
    levels = np.array([10, -10, 5, -5, 0])
    if k % 512:
        return np.exp2(np.random.permutation(np.resize(levels, k // 32))).repeat(32)
    a = np.empty((k // 512, 16))
    for p in range(k // 512):
        a[p, :8] = np.random.permutation(np.resize(levels, 8))
        for g in range(8):
            far = levels[np.abs(levels - a[p, g]) >= 10]
            a[p, g + 8] = far[np.random.randint(len(far))]
    return np.exp2(a.ravel()).repeat(32)


def f64(x):
    return np.asarray(x).astype(np.float64)


def striped(idx):
    return np.tile(idx.reshape(-1, 16).T, (8, 1)).astype(np.uint16)


def unstriped(offs):
    return offs[:16].T.reshape(-1).astype(np.int64)


def pack_weight(w):
    k, n = w.shape
    w = f64(np.asarray(w, np.float32).astype(ml_dtypes.bfloat16)).reshape(k // 32, 32, n)
    amax = np.abs(w).max(1)
    byte = np.clip(np.where(amax > 0, np.frexp(amax)[1] - 1 + 127 - 7, 1), 1, 254)
    scaled = (w * np.exp2(127.0 - byte)[:, None, :]).reshape(k, n).astype(np.float32)
    words = np.ascontiguousarray(scaled.reshape(k // 512, 128, 4, n).transpose(0, 1, 3, 2)).astype(ml_dtypes.float8_e4m3fn).view(np.uint8)
    return words, np.ascontiguousarray(byte.astype(np.uint8).reshape(k // 512, 16, n))


def unpack_weight(words, scales):
    g, p, n, _ = words.shape
    vals = np.ascontiguousarray(words).view(ml_dtypes.float8_e4m3fn).astype(np.float64) * np.repeat(np.exp2(scales.astype(np.float64) - 127.0), 8, axis=1)[..., None]
    return vals.transpose(0, 1, 3, 2).reshape(g * 512, n)


K, T, S, N, U = 512, 1024, 512, 256, 1024


def setup_inputs():
    n = np.random.standard_normal
    s = mx_kscale(K)[:, None]
    packed_w1 = pack_weight(n((K, N)) / np.sqrt(K) / s)
    return {
        "xT": (n((K, T)) * s).astype(np.float32),
        "mem": n((N, U)).astype(np.float32),
        "w1_words": packed_w1[0],
        "w1_scales": packed_w1[1],
        "offs": striped(np.random.permutation(T)[:S]),
        "slot": striped(np.random.permutation(U)[:S]),
    }


def reference(xT, mem, w1_words, w1_scales, offs, slot):
    xq = mxq(f64(xT)[:, unstriped(offs)], 0, "e4m3")
    y = unpack_weight(w1_words, w1_scales).T @ xq
    out = f64(mem).copy()
    out[:, unstriped(slot)] = np.minimum(f64(mem)[:, unstriped(slot)], y)
    return out

@@ -1,0 +1,79 @@
+import concourse.mybir as mybir
+
+K, T, S, N, U = 512, 1024, 512, 256, 1024
+P = 128
+F32, BF16 = mybir.dt.float32, mybir.dt.bfloat16
+U32, I32, U16, U8 = mybir.dt.uint32, mybir.dt.int32, mybir.dt.uint16, mybir.dt.uint8
+FP8X4 = mybir.dt.float8_e4m3fn_x4
+FLOPS = 2 * K * S * N
+HALF = T // 2
+VEC_SHARE = 320
+
+
+def tile_picked_idxput_min_e_kernel(tc, xT, mem, w1_words, w1_scales, offs, slot, out):
+    nc = tc.nc
+    with tc.tile_pool(name="keep", bufs=1) as keep, tc.psum_pool(name="psum", bufs=1) as psum:
+        offs_t = keep.tile([P, S // 16], U16, name="offs_t")
+        slot_t = keep.tile([P, S // 16], U16, name="slot_t")
+        w_scales = keep.tile([P, N], U8, name="w_scales", align_bytes=64)
+        w_codes = keep.tile([P, N], U32, name="w_codes", align_bytes=64)
+        nc.gpsimd.memset(w_scales[:].bitcast(I32), 0)
+
+        x_rows = xT.rearrange("(p j) t -> p j t", j=4)
+        raw = [[keep.tile([P, 2, HALF], F32, name="raw%d%d" % (u, h)) for h in range(2)] for u in range(2)]
+        store = [keep.tile([P, U], F32, name="store%d" % b) for b in range(2)]
+        nc.sync.dma_start(offs_t[:], offs)
+        for u in range(2):
+            for h in range(2):
+                nc.sync.dma_start(raw[u][h][:], x_rows[:, 2 * u : 2 * u + 2, h * HALF : (h + 1) * HALF])
+        nc.sync.dma_start(slot_t[:], slot)
+        nc.sync.dma_start(store[0][:], mem[0:P, :])
+        nc.sync.dma_start(w_codes[:].bitcast(I32), w1_words[0].rearrange("p n t -> p (n t)").bitcast(I32))
+        for q in range(4):
+            nc.sync.dma_start(w_scales[32 * q : 32 * q + 4, :].bitcast(I32), w1_scales[0, 4 * q : 4 * q + 4, :].bitcast(I32))
+        nc.sync.dma_start(store[1][:], mem[P : 2 * P, :])
+
+        pairs = [keep.tile([P, T, 2], BF16, name="pairs%d" % u) for u in range(2)]
+        picked = keep.tile([P, S, 2], U32, name="picked", align_bytes=64)
+
+        def cast(copy, u, h, c0, c1):
+            copy(pairs[u][:, h * HALF + c0 : h * HALF + c1, :], raw[u][h][:, :, c0:c1].rearrange("p j t -> p t j"))
+
+        def pick(u):
+            window = pairs[u][:].rearrange("p t j -> p (t j)").bitcast(U32)
+            nc.vector.tensor_copy(picked[:, :, u], window.indirect(offs_t[:]))
+
+        cast(nc.scalar.copy, 0, 0, 0, HALF)
+        cast(nc.scalar.copy, 0, 1, 0, HALF)
+        pick(0)
+        cast(nc.scalar.copy, 1, 0, 0, HALF)
+        cast(nc.vector.tensor_copy, 1, 1, 0, VEC_SHARE)
+        cast(nc.scalar.copy, 1, 1, VEC_SHARE, HALF)
+        pick(1)
+
+        old = [keep.tile([P, S], F32, name="old%d" % b) for b in range(2)]
+        new = [keep.tile([P, S], F32, name="new%d" % b) for b in range(2)]
+        x_codes = keep.tile([P, S], U32, name="x_codes", align_bytes=64)
+        x_scales = keep.tile([P, S], U8, name="x_scales", align_bytes=64)
+        nc.vector.tensor_copy(old[0][:], store[0][:].indirect(slot_t[:]))
+        nc.vector.quantize_mx(
+            out=x_codes[:].bitcast(FP8X4),
+            scales=x_scales[:],
+            in_=picked[:].rearrange("p s u -> p (s u)").bitcast(BF16),
+        )
+        nc.vector.tensor_copy(old[1][:], store[1][:].indirect(slot_t[:]))
+        for b in range(2):
+            y = psum.tile([P, S], F32, name="y%d" % b)
+            cols = slice(b * P, (b + 1) * P)
+            nc.tensor.matmul_mx(
+                out=y[:],
+                lhsT=w_codes[:, cols].bitcast(FP8X4),
+                lhsT_scale=w_scales[:, cols],
+                rhs=x_codes[:].bitcast(FP8X4),
+                rhs_scale=x_scales[:],
+                start=True,
+                stop=True,
+            )
+            nc.vector.tensor_tensor(new[b][:], y[:], old[b][:], mybir.AluOpType.min)
+            nc.vector.tensor_copy(store[b][:].indirect(slot_t[:]), new[b][:])
+            nc.sync.dma_start(out[cols, :], store[b][:])

@@ -7,7 +7,7 @@ U32, I32, U16, U8 = mybir.dt.uint32, mybir.dt.int32, mybir.dt.uint16, mybir.dt.u
 FP8X4 = mybir.dt.float8_e4m3fn_x4
 FLOPS = 2 * K * S * N
 HALF = T // 2
-VEC_SHARE = 320
+VEC_SHARE = 352
 
 
 def tile_picked_idxput_min_e_kernel(tc, xT, mem, w1_words, w1_scales, offs, slot, out):
@@ -22,36 +22,40 @@ def tile_picked_idxput_min_e_kernel(tc, xT, mem, w1_words, w1_scales, offs, slot
         x_rows = xT.rearrange("(p j) t -> p j t", j=4)
         raw = [[keep.tile([P, 2, HALF], F32, name="raw%d%d" % (u, h)) for h in range(2)] for u in range(2)]
         store = [keep.tile([P, U], F32, name="store%d" % b) for b in range(2)]
-        nc.sync.dma_start(offs_t[:], offs)
         for u in range(2):
             for h in range(2):
                 nc.sync.dma_start(raw[u][h][:], x_rows[:, 2 * u : 2 * u + 2, h * HALF : (h + 1) * HALF])
+            if u == 0:
+                nc.sync.dma_start(offs_t[:], offs)
         nc.sync.dma_start(slot_t[:], slot)
         nc.sync.dma_start(store[0][:], mem[0:P, :])
+        nc.sync.dma_start(store[1][:], mem[P : 2 * P, :])
         nc.sync.dma_start(w_codes[:].bitcast(I32), w1_words[0].rearrange("p n t -> p (n t)").bitcast(I32))
         for q in range(4):
             nc.sync.dma_start(w_scales[32 * q : 32 * q + 4, :].bitcast(I32), w1_scales[0, 4 * q : 4 * q + 4, :].bitcast(I32))
-        nc.sync.dma_start(store[1][:], mem[P : 2 * P, :])
 
         pairs = [keep.tile([P, T, 2], BF16, name="pairs%d" % u) for u in range(2)]
-        picked = keep.tile([P, S, 2], U32, name="picked", align_bytes=64)
+        picked = keep.tile([P, 2, S], U32, name="picked")
+        woven = keep.tile([P, S, 2], U32, name="woven", tag="woven", align_bytes=64)
 
         def cast(copy, u, h, c0, c1):
             copy(pairs[u][:, h * HALF + c0 : h * HALF + c1, :], raw[u][h][:, :, c0:c1].rearrange("p j t -> p t j"))
 
-        def pick(u):
+        def pick(u, s0, s1):
             window = pairs[u][:].rearrange("p t j -> p (t j)").bitcast(U32)
-            nc.vector.tensor_copy(picked[:, :, u], window.indirect(offs_t[:]))
+            nc.vector.tensor_copy(picked[:, u, s0:s1], window.indirect(offs_t[:, s0 // 16 : s1 // 16]))
 
         cast(nc.scalar.copy, 0, 0, 0, HALF)
-        cast(nc.scalar.copy, 0, 1, 0, HALF)
-        pick(0)
+        cast(nc.vector.tensor_copy, 0, 1, 0, HALF)
+        pick(0, 0, S)
         cast(nc.scalar.copy, 1, 0, 0, HALF)
         cast(nc.vector.tensor_copy, 1, 1, 0, VEC_SHARE)
         cast(nc.scalar.copy, 1, 1, VEC_SHARE, HALF)
-        pick(1)
+        for s0 in (0, S // 2):
+            pick(1, s0, s0 + S // 2)
+            nc.scalar.copy(woven[:, s0 : s0 + S // 2, :], picked[:, :, s0 : s0 + S // 2].rearrange("p u s -> p s u"))
 
-        old = [keep.tile([P, S], F32, name="old%d" % b) for b in range(2)]
+        old = [keep.tile([P, S], F32, name="old0")]
         new = [keep.tile([P, S], F32, name="new%d" % b) for b in range(2)]
         x_codes = keep.tile([P, S], U32, name="x_codes", align_bytes=64)
         x_scales = keep.tile([P, S], U8, name="x_scales", align_bytes=64)
@@ -59,8 +63,9 @@ def tile_picked_idxput_min_e_kernel(tc, xT, mem, w1_words, w1_scales, offs, slot
         nc.vector.quantize_mx(
             out=x_codes[:].bitcast(FP8X4),
             scales=x_scales[:],
-            in_=picked[:].rearrange("p s u -> p (s u)").bitcast(BF16),
+            in_=woven[:].rearrange("p s u -> p (s u)").bitcast(BF16),
         )
+        old.append(keep.tile([P, S], F32, name="old1", tag="woven", align_bytes=64))
         nc.vector.tensor_copy(old[1][:], store[1][:].indirect(slot_t[:]))
         for b in range(2):
             y = psum.tile([P, S], F32, name="y%d" % b)
@@ -75,5 +80,6 @@ def tile_picked_idxput_min_e_kernel(tc, xT, mem, w1_words, w1_scales, offs, slot
                 stop=True,
             )
             nc.vector.tensor_tensor(new[b][:], y[:], old[b][:], mybir.AluOpType.min)
+        for b in range(2):
             nc.vector.tensor_copy(store[b][:].indirect(slot_t[:]), new[b][:])
-            nc.sync.dma_start(out[cols, :], store[b][:])
+            nc.sync.dma_start(out[b * P : (b + 1) * P, :], store[b][:])

@@ -6,8 +6,8 @@ F32, BF16 = mybir.dt.float32, mybir.dt.bfloat16
 U32, I32, U16, U8 = mybir.dt.uint32, mybir.dt.int32, mybir.dt.uint16, mybir.dt.uint8
 FP8X4 = mybir.dt.float8_e4m3fn_x4
 FLOPS = 2 * K * S * N
-HALF = T // 2
-VEC_SHARE = 352
+HALF = S // 2
+SCALAR_SHARE = 128
 
 
 def tile_picked_idxput_min_e_kernel(tc, xT, mem, w1_words, w1_scales, offs, slot, out):
@@ -20,40 +20,39 @@ def tile_picked_idxput_min_e_kernel(tc, xT, mem, w1_words, w1_scales, offs, slot
         nc.gpsimd.memset(w_scales[:].bitcast(I32), 0)
 
         x_rows = xT.rearrange("(p j) t -> p j t", j=4)
-        raw = [[keep.tile([P, 2, HALF], F32, name="raw%d%d" % (u, h)) for h in range(2)] for u in range(2)]
+        raw = [keep.tile([P, T], F32, name="raw%d" % j) for j in range(4)]
         store = [keep.tile([P, U], F32, name="store%d" % b) for b in range(2)]
-        for u in range(2):
-            for h in range(2):
-                nc.sync.dma_start(raw[u][h][:], x_rows[:, 2 * u : 2 * u + 2, h * HALF : (h + 1) * HALF])
-            if u == 0:
+        for j in range(4):
+            nc.sync.dma_start(raw[j][:], x_rows[:, j, :])
+            if j == 0:
                 nc.sync.dma_start(offs_t[:], offs)
-        nc.sync.dma_start(slot_t[:], slot)
+            if j == 2:
+                nc.sync.dma_start(slot_t[:], slot)
         nc.sync.dma_start(store[0][:], mem[0:P, :])
         nc.sync.dma_start(store[1][:], mem[P : 2 * P, :])
         nc.sync.dma_start(w_codes[:].bitcast(I32), w1_words[0].rearrange("p n t -> p (n t)").bitcast(I32))
         for q in range(4):
             nc.sync.dma_start(w_scales[32 * q : 32 * q + 4, :].bitcast(I32), w1_scales[0, 4 * q : 4 * q + 4, :].bitcast(I32))
 
-        pairs = [keep.tile([P, T, 2], BF16, name="pairs%d" % u) for u in range(2)]
-        picked = keep.tile([P, 2, S], U32, name="picked")
-        woven = keep.tile([P, S, 2], U32, name="woven", tag="woven", align_bytes=64)
+        picked = [keep.tile([P, 2, S], dtype, name="picked%d" % u) for u, dtype in enumerate((BF16, F32))]
+        woven = keep.tile([P, S, 4], BF16, name="woven", tag="woven", align_bytes=64)
 
-        def cast(copy, u, h, c0, c1):
-            copy(pairs[u][:, h * HALF + c0 : h * HALF + c1, :], raw[u][h][:, :, c0:c1].rearrange("p j t -> p t j"))
+        def pick(j, s0, s1):
+            nc.vector.tensor_copy(picked[j // 2][:, j % 2, s0:s1], raw[j][:].indirect(offs_t[:, s0 // 16 : s1 // 16]))
 
-        def pick(u, s0, s1):
-            window = pairs[u][:].rearrange("p t j -> p (t j)").bitcast(U32)
-            nc.vector.tensor_copy(picked[:, u, s0:s1], window.indirect(offs_t[:, s0 // 16 : s1 // 16]))
+        def weave(u, s0, s1):
+            nc.scalar.activation(woven[:, s0:s1, 2 * u : 2 * u + 2], picked[u][:, :, s0:s1].rearrange("p j s -> p s j"), mybir.ActivationFunctionType.Copy)
 
-        cast(nc.scalar.copy, 0, 0, 0, HALF)
-        cast(nc.vector.tensor_copy, 0, 1, 0, HALF)
-        pick(0, 0, S)
-        cast(nc.scalar.copy, 1, 0, 0, HALF)
-        cast(nc.vector.tensor_copy, 1, 1, 0, VEC_SHARE)
-        cast(nc.scalar.copy, 1, 1, VEC_SHARE, HALF)
-        for s0 in (0, S // 2):
-            pick(1, s0, s0 + S // 2)
-            nc.scalar.copy(woven[:, s0 : s0 + S // 2, :], picked[:, :, s0 : s0 + S // 2].rearrange("p u s -> p s u"))
+        rounded = keep.tile([P, T], BF16, name="rounded")
+        nc.scalar.copy(rounded[:], raw[0][:])
+        nc.scalar.activation(picked[0][:, 0, S - SCALAR_SHARE :], rounded[:].indirect(offs_t[:, (S - SCALAR_SHARE) // 16 :]), mybir.ActivationFunctionType.Copy)
+        pick(0, 0, S - SCALAR_SHARE)
+        pick(1, 0, S)
+        weave(0, 0, S)
+        pick(2, 0, S)
+        for s0 in (0, HALF):
+            pick(3, s0, s0 + HALF)
+            weave(1, s0, s0 + HALF)
 
         old = [keep.tile([P, S], F32, name="old0")]
         new = [keep.tile([P, S], F32, name="new%d" % b) for b in range(2)]
@@ -63,7 +62,7 @@ def tile_picked_idxput_min_e_kernel(tc, xT, mem, w1_words, w1_scales, offs, slot
         nc.vector.quantize_mx(
             out=x_codes[:].bitcast(FP8X4),
             scales=x_scales[:],
-            in_=woven[:].rearrange("p s u -> p (s u)").bitcast(BF16),
+            in_=woven[:].rearrange("p s j -> p (s j)"),
         )
         old.append(keep.tile([P, S], F32, name="old1", tag="woven", align_bytes=64))
         nc.vector.tensor_copy(old[1][:], store[1][:].indirect(slot_t[:]))

@@ -6,8 +6,7 @@ F32, BF16 = mybir.dt.float32, mybir.dt.bfloat16
 U32, I32, U16, U8 = mybir.dt.uint32, mybir.dt.int32, mybir.dt.uint16, mybir.dt.uint8
 FP8X4 = mybir.dt.float8_e4m3fn_x4
 FLOPS = 2 * K * S * N
-HALF = S // 2
-SCALAR_SHARE = 128
+SCALAR_SHARE = 192
 
 
 def tile_picked_idxput_min_e_kernel(tc, xT, mem, w1_words, w1_scales, offs, slot, out):
@@ -34,25 +33,26 @@ def tile_picked_idxput_min_e_kernel(tc, xT, mem, w1_words, w1_scales, offs, slot
         for q in range(4):
             nc.sync.dma_start(w_scales[32 * q : 32 * q + 4, :].bitcast(I32), w1_scales[0, 4 * q : 4 * q + 4, :].bitcast(I32))
 
-        picked = [keep.tile([P, 2, S], dtype, name="picked%d" % u) for u, dtype in enumerate((BF16, F32))]
+        picked = keep.tile([P, 2, S], F32, name="picked")
         woven = keep.tile([P, S, 4], BF16, name="woven", tag="woven", align_bytes=64)
+        split = S - SCALAR_SHARE
+
+        for j in range(2):
+            rounded = keep.tile([P, T], BF16, name="rounded%d" % j)
+            nc.scalar.copy(rounded[:], raw[j][:])
+            nc.scalar.activation(woven[:, split:, j], rounded[:].indirect(offs_t[:, split // 16 :]), mybir.ActivationFunctionType.Copy)
+            nc.vector.tensor_copy(woven[:, :split, j], raw[j][:].indirect(offs_t[:, : split // 16]))
 
         def pick(j, s0, s1):
-            nc.vector.tensor_copy(picked[j // 2][:, j % 2, s0:s1], raw[j][:].indirect(offs_t[:, s0 // 16 : s1 // 16]))
+            nc.vector.tensor_copy(picked[:, j - 2, s0:s1], raw[j][:].indirect(offs_t[:, s0 // 16 : s1 // 16]))
 
         def weave(u, s0, s1):
-            nc.scalar.activation(woven[:, s0:s1, 2 * u : 2 * u + 2], picked[u][:, :, s0:s1].rearrange("p j s -> p s j"), mybir.ActivationFunctionType.Copy)
+            nc.scalar.activation(woven[:, s0:s1, 2:4], picked[:, :, s0:s1].rearrange("p j s -> p s j"), mybir.ActivationFunctionType.Copy)
 
-        rounded = keep.tile([P, T], BF16, name="rounded")
-        nc.scalar.copy(rounded[:], raw[0][:])
-        nc.scalar.activation(picked[0][:, 0, S - SCALAR_SHARE :], rounded[:].indirect(offs_t[:, (S - SCALAR_SHARE) // 16 :]), mybir.ActivationFunctionType.Copy)
-        pick(0, 0, S - SCALAR_SHARE)
-        pick(1, 0, S)
-        weave(0, 0, S)
         pick(2, 0, S)
-        for s0 in (0, HALF):
-            pick(3, s0, s0 + HALF)
-            weave(1, s0, s0 + HALF)
+        for s0, s1 in ((0, 128), (128, 320), (320, S)):
+            pick(3, s0, s1)
+            weave(1, s0, s1)
 
         old = [keep.tile([P, S], F32, name="old0")]
         new = [keep.tile([P, S], F32, name="new%d" % b) for b in range(2)]

@@ -5,8 +5,10 @@ P = 128
 F32, BF16 = mybir.dt.float32, mybir.dt.bfloat16
 U32, I32, U16, U8 = mybir.dt.uint32, mybir.dt.int32, mybir.dt.uint16, mybir.dt.uint8
 FP8X4 = mybir.dt.float8_e4m3fn_x4
+COPY = mybir.ActivationFunctionType.Copy
+MIN = mybir.AluOpType.min
 FLOPS = 2 * K * S * N
-SCALAR_SHARE = 192
+H = S // 2
 
 
 def tile_picked_idxput_min_e_kernel(tc, xT, mem, w1_words, w1_scales, offs, slot, out):
@@ -25,60 +27,61 @@ def tile_picked_idxput_min_e_kernel(tc, xT, mem, w1_words, w1_scales, offs, slot
             nc.sync.dma_start(raw[j][:], x_rows[:, j, :])
             if j == 0:
                 nc.sync.dma_start(offs_t[:], offs)
-            if j == 2:
-                nc.sync.dma_start(slot_t[:], slot)
+        nc.sync.dma_start(slot_t[:], slot)
         nc.sync.dma_start(store[0][:], mem[0:P, :])
-        nc.sync.dma_start(store[1][:], mem[P : 2 * P, :])
         nc.sync.dma_start(w_codes[:].bitcast(I32), w1_words[0].rearrange("p n t -> p (n t)").bitcast(I32))
         for q in range(4):
             nc.sync.dma_start(w_scales[32 * q : 32 * q + 4, :].bitcast(I32), w1_scales[0, 4 * q : 4 * q + 4, :].bitcast(I32))
+        nc.sync.dma_start(store[1][:], mem[P : 2 * P, :])
 
-        picked = keep.tile([P, 2, S], F32, name="picked")
-        woven = keep.tile([P, S, 4], BF16, name="woven", tag="woven", align_bytes=64)
-        split = S - SCALAR_SHARE
-
-        for j in range(2):
+        woven = [keep.tile([P, H, 4], BF16, name="woven%d" % h, align_bytes=64) for h in range(2)]
+        for j in range(4):
+            nc.vector.tensor_copy(woven[0][:, :, j], raw[j][:].indirect(offs_t[:, : H // 16]))
             rounded = keep.tile([P, T], BF16, name="rounded%d" % j)
             nc.scalar.copy(rounded[:], raw[j][:])
-            nc.scalar.activation(woven[:, split:, j], rounded[:].indirect(offs_t[:, split // 16 :]), mybir.ActivationFunctionType.Copy)
-            nc.vector.tensor_copy(woven[:, :split, j], raw[j][:].indirect(offs_t[:, : split // 16]))
+            nc.scalar.activation(woven[1][:, :, j], rounded[:].indirect(offs_t[:, H // 16 :]), COPY)
 
-        def pick(j, s0, s1):
-            nc.vector.tensor_copy(picked[:, j - 2, s0:s1], raw[j][:].indirect(offs_t[:, s0 // 16 : s1 // 16]))
+        y0 = [psum.tile([P, H], F32, name="y0_%d" % h) for h in range(2)]
+        y1 = psum.tile([P, S], F32, name="y1")
 
-        def weave(u, s0, s1):
-            nc.scalar.activation(woven[:, s0:s1, 2:4], picked[:, :, s0:s1].rearrange("p j s -> p s j"), mybir.ActivationFunctionType.Copy)
+        def project(h, codes):
+            scales = keep.tile([P, H], U8, name="x_scales%d" % h, align_bytes=64)
+            nc.vector.quantize_mx(out=codes[:].bitcast(FP8X4), scales=scales[:], in_=woven[h][:].rearrange("p s j -> p (s j)"))
+            for b, y in enumerate((y0[h][:], y1[:, h * H : (h + 1) * H])):
+                cols = slice(b * P, (b + 1) * P)
+                nc.tensor.matmul_mx(
+                    out=y,
+                    lhsT=w_codes[:, cols].bitcast(FP8X4),
+                    lhsT_scale=w_scales[:, cols],
+                    rhs=codes[:].bitcast(FP8X4),
+                    rhs_scale=scales[:],
+                    start=True,
+                    stop=True,
+                )
 
-        pick(2, 0, S)
-        for s0, s1 in ((0, 128), (128, 320), (320, S)):
-            pick(3, s0, s1)
-            weave(1, s0, s1)
+        def look_up(dst, b, s0, s1):
+            nc.vector.tensor_copy(dst, store[b][:].indirect(slot_t[:, s0 // 16 : s1 // 16]))
 
-        old = [keep.tile([P, S], F32, name="old0")]
-        new = [keep.tile([P, S], F32, name="new%d" % b) for b in range(2)]
-        x_codes = keep.tile([P, S], U32, name="x_codes", align_bytes=64)
-        x_scales = keep.tile([P, S], U8, name="x_scales", align_bytes=64)
-        nc.vector.tensor_copy(old[0][:], store[0][:].indirect(slot_t[:]))
-        nc.vector.quantize_mx(
-            out=x_codes[:].bitcast(FP8X4),
-            scales=x_scales[:],
-            in_=woven[:].rearrange("p s j -> p (s j)"),
-        )
-        old.append(keep.tile([P, S], F32, name="old1", tag="woven", align_bytes=64))
-        nc.vector.tensor_copy(old[1][:], store[1][:].indirect(slot_t[:]))
-        for b in range(2):
-            y = psum.tile([P, S], F32, name="y%d" % b)
-            cols = slice(b * P, (b + 1) * P)
-            nc.tensor.matmul_mx(
-                out=y[:],
-                lhsT=w_codes[:, cols].bitcast(FP8X4),
-                lhsT_scale=w_scales[:, cols],
-                rhs=x_codes[:].bitcast(FP8X4),
-                rhs_scale=x_scales[:],
-                start=True,
-                stop=True,
-            )
-            nc.vector.tensor_tensor(new[b][:], y[:], old[b][:], mybir.AluOpType.min)
-        for b in range(2):
-            nc.vector.tensor_copy(store[b][:].indirect(slot_t[:]), new[b][:])
-            nc.sync.dma_start(out[b * P : (b + 1) * P, :], store[b][:])
+        def put_back(b, s0, s1, src):
+            nc.vector.tensor_copy(store[b][:].indirect(slot_t[:, s0 // 16 : s1 // 16]), src)
+
+        project(0, keep.tile([P, H], U32, name="x_codes0", align_bytes=64))
+        old0a = keep.tile([P, H], F32, name="old0a", tag="t1", align_bytes=64)
+        old0b = keep.tile([P, H], F32, name="old0b")
+        look_up(old0a[:], 0, 0, H)
+        look_up(old0b[:], 0, H, S)
+        new0a = keep.tile([P, H], F32, name="new0a", tag="t2")
+        nc.vector.tensor_tensor(new0a[:], y0[0][:], old0a[:], MIN)
+        put_back(0, 0, H, new0a[:])
+
+        project(1, keep.tile([P, H], U32, name="x_codes1", tag="t1", align_bytes=64))
+        old1 = keep.tile([P, S], F32, name="old1", tag="t2")
+        look_up(old1[:], 1, 0, S)
+        new0b = keep.tile([P, H], F32, name="new0b")
+        new1 = keep.tile([P, S], F32, name="new1")
+        nc.vector.tensor_tensor(new0b[:], y0[1][:], old0b[:], MIN)
+        nc.vector.tensor_tensor(new1[:], y1[:], old1[:], MIN)
+        put_back(0, H, S, new0b[:])
+        nc.sync.dma_start(out[0:P, :], store[0][:])
+        put_back(1, 0, S, new1[:])
+        nc.sync.dma_start(out[P : 2 * P, :], store[1][:])

@@ -16,37 +16,42 @@ def tile_picked_idxput_min_e_kernel(tc, xT, mem, w1_words, w1_scales, offs, slot
     with tc.tile_pool(name="keep", bufs=1) as keep, tc.psum_pool(name="psum", bufs=1) as psum:
         offs_t = keep.tile([P, S // 16], U16, name="offs_t")
         slot_t = keep.tile([P, S // 16], U16, name="slot_t")
-        w_scales = keep.tile([P, N], U8, name="w_scales", align_bytes=64)
         w_codes = keep.tile([P, N], U32, name="w_codes", align_bytes=64)
-        nc.gpsimd.memset(w_scales[:].bitcast(I32), 0)
 
         x_rows = xT.rearrange("(p j) t -> p j t", j=4)
-        raw = [keep.tile([P, T], F32, name="raw%d" % j) for j in range(4)]
-        store = [keep.tile([P, U], F32, name="store%d" % b) for b in range(2)]
-        for j in range(4):
-            nc.sync.dma_start(raw[j][:], x_rows[:, j, :])
-            if j == 0:
-                nc.sync.dma_start(offs_t[:], offs)
+        raw = [keep.tile([P, T], F32, name="raw%d" % j, align_bytes=64) for j in range(4)]
+        store = [keep.tile([P, U], F32, name="store0")]
+        nc.sync.dma_start(offs_t[:], offs)
         nc.sync.dma_start(slot_t[:], slot)
-        nc.sync.dma_start(store[0][:], mem[0:P, :])
-        nc.sync.dma_start(w_codes[:].bitcast(I32), w1_words[0].rearrange("p n t -> p (n t)").bitcast(I32))
-        for q in range(4):
-            nc.sync.dma_start(w_scales[32 * q : 32 * q + 4, :].bitcast(I32), w1_scales[0, 4 * q : 4 * q + 4, :].bitcast(I32))
-        nc.sync.dma_start(store[1][:], mem[P : 2 * P, :])
+        for j in range(4):
+            nc.scalar.dma_start(raw[j][:], x_rows[:, j, :])
+        nc.scalar.dma_start(store[0][:], mem[0:P, :])
+        nc.scalar.dma_start(w_codes[:].bitcast(I32), w1_words[0].rearrange("p n t -> p (n t)").bitcast(I32))
 
         woven = [keep.tile([P, H, 4], BF16, name="woven%d" % h, align_bytes=64) for h in range(2)]
         for j in range(4):
-            nc.vector.tensor_copy(woven[0][:, :, j], raw[j][:].indirect(offs_t[:, : H // 16]))
+            for s0, s1 in ((0, H),) if j < 3 else ((0, H // 2), (H // 2, H)):
+                nc.vector.tensor_copy(woven[0][:, s0:s1, j], raw[j][:].indirect(offs_t[:, s0 // 16 : s1 // 16]))
             rounded = keep.tile([P, T], BF16, name="rounded%d" % j)
             nc.scalar.copy(rounded[:], raw[j][:])
             nc.scalar.activation(woven[1][:, :, j], rounded[:].indirect(offs_t[:, H // 16 :]), COPY)
+
+        w_scales = keep.tile([P, N], U8, name="w_scales", tag="raw0", align_bytes=64)
+        nc.gpsimd.memset(w_scales[:].bitcast(I32), 0)
+        for q in range(4):
+            nc.sync.dma_start(w_scales[32 * q : 32 * q + 4, :].bitcast(I32), w1_scales[0, 4 * q : 4 * q + 4, :].bitcast(I32))
+        store.append(keep.tile([P, U], F32, name="store1", tag="raw1", align_bytes=64))
+        nc.sync.dma_start(store[1][:], mem[P : 2 * P, :])
 
         y0 = [psum.tile([P, H], F32, name="y0_%d" % h) for h in range(2)]
         y1 = psum.tile([P, S], F32, name="y1")
 
         def project(h, codes):
             scales = keep.tile([P, H], U8, name="x_scales%d" % h, align_bytes=64)
-            nc.vector.quantize_mx(out=codes[:].bitcast(FP8X4), scales=scales[:], in_=woven[h][:].rearrange("p s j -> p (s j)"))
+            for s0, s1 in ((0, H // 2), (H // 2, H)) if h == 0 else ((0, H),):
+                nc.vector.quantize_mx(
+                    out=codes[:, s0:s1].bitcast(FP8X4), scales=scales[:, s0:s1], in_=woven[h][:, s0:s1, :].rearrange("p s j -> p (s j)")
+                )
             for b, y in enumerate((y0[h][:], y1[:, h * H : (h + 1) * H])):
                 cols = slice(b * P, (b + 1) * P)
                 nc.tensor.matmul_mx(

@@ -16,17 +16,23 @@ def tile_picked_idxput_min_e_kernel(tc, xT, mem, w1_words, w1_scales, offs, slot
     with tc.tile_pool(name="keep", bufs=1) as keep, tc.psum_pool(name="psum", bufs=1) as psum:
         offs_t = keep.tile([P, S // 16], U16, name="offs_t")
         slot_t = keep.tile([P, S // 16], U16, name="slot_t")
+        w_scales = keep.tile([P, N], U8, name="w_scales", align_bytes=64)
         w_codes = keep.tile([P, N], U32, name="w_codes", align_bytes=64)
+        nc.gpsimd.memset(w_scales[:].bitcast(I32), 0)
+        for q in range(4):
+            nc.gpsimd.dma_start(w_scales[32 * q : 32 * q + 4, :].bitcast(I32), w1_scales[0, 4 * q : 4 * q + 4, :].bitcast(I32))
 
         x_rows = xT.rearrange("(p j) t -> p j t", j=4)
-        raw = [keep.tile([P, T], F32, name="raw%d" % j, align_bytes=64) for j in range(4)]
-        store = [keep.tile([P, U], F32, name="store0")]
-        nc.sync.dma_start(offs_t[:], offs)
-        nc.sync.dma_start(slot_t[:], slot)
+        raw = [keep.tile([P, T], F32, name="raw%d" % j) for j in range(4)]
+        store = [keep.tile([P, U], F32, name="store%d" % b) for b in range(2)]
         for j in range(4):
-            nc.scalar.dma_start(raw[j][:], x_rows[:, j, :])
-        nc.scalar.dma_start(store[0][:], mem[0:P, :])
-        nc.scalar.dma_start(w_codes[:].bitcast(I32), w1_words[0].rearrange("p n t -> p (n t)").bitcast(I32))
+            nc.sync.dma_start(raw[j][:], x_rows[:, j, :])
+            if j == 0:
+                nc.sync.dma_start(offs_t[:], offs)
+        nc.sync.dma_start(slot_t[:], slot)
+        nc.sync.dma_start(store[0][:], mem[0:P, :])
+        nc.sync.dma_start(store[1][:], mem[P : 2 * P, :])
+        nc.sync.dma_start(w_codes[:].bitcast(I32), w1_words[0].rearrange("p n t -> p (n t)").bitcast(I32))
 
         woven = [keep.tile([P, H, 4], BF16, name="woven%d" % h, align_bytes=64) for h in range(2)]
         for j in range(4):
@@ -36,15 +42,10 @@ def tile_picked_idxput_min_e_kernel(tc, xT, mem, w1_words, w1_scales, offs, slot
             nc.scalar.copy(rounded[:], raw[j][:])
             nc.scalar.activation(woven[1][:, :, j], rounded[:].indirect(offs_t[:, H // 16 :]), COPY)
 
-        w_scales = keep.tile([P, N], U8, name="w_scales", tag="raw0", align_bytes=64)
-        nc.gpsimd.memset(w_scales[:].bitcast(I32), 0)
-        for q in range(4):
-            nc.sync.dma_start(w_scales[32 * q : 32 * q + 4, :].bitcast(I32), w1_scales[0, 4 * q : 4 * q + 4, :].bitcast(I32))
-        store.append(keep.tile([P, U], F32, name="store1", tag="raw1", align_bytes=64))
-        nc.sync.dma_start(store[1][:], mem[P : 2 * P, :])
-
-        y0 = [psum.tile([P, H], F32, name="y0_%d" % h) for h in range(2)]
-        y1 = psum.tile([P, S], F32, name="y1")
+        ya = [psum.tile([P, H], F32, name="ya%d" % b) for b in range(2)]
+        yb = psum.tile([P, 2, H], F32, name="yb")
+        y0 = [ya[0][:], yb[:, 0, :]]
+        y1 = [ya[1][:], yb[:, 1, :]]
 
         def project(h, codes):
             scales = keep.tile([P, H], U8, name="x_scales%d" % h, align_bytes=64)
@@ -52,7 +53,7 @@ def tile_picked_idxput_min_e_kernel(tc, xT, mem, w1_words, w1_scales, offs, slot
                 nc.vector.quantize_mx(
                     out=codes[:, s0:s1].bitcast(FP8X4), scales=scales[:, s0:s1], in_=woven[h][:, s0:s1, :].rearrange("p s j -> p (s j)")
                 )
-            for b, y in enumerate((y0[h][:], y1[:, h * H : (h + 1) * H])):
+            for b, y in enumerate((y0[h], y1[h])):
                 cols = slice(b * P, (b + 1) * P)
                 nc.tensor.matmul_mx(
                     out=y,
@@ -70,23 +71,22 @@ def tile_picked_idxput_min_e_kernel(tc, xT, mem, w1_words, w1_scales, offs, slot
         def put_back(b, s0, s1, src):
             nc.vector.tensor_copy(store[b][:].indirect(slot_t[:, s0 // 16 : s1 // 16]), src)
 
-        project(0, keep.tile([P, H], U32, name="x_codes0", align_bytes=64))
-        old0a = keep.tile([P, H], F32, name="old0a", tag="t1", align_bytes=64)
-        old0b = keep.tile([P, H], F32, name="old0b")
-        look_up(old0a[:], 0, 0, H)
-        look_up(old0b[:], 0, H, S)
-        new0a = keep.tile([P, H], F32, name="new0a", tag="t2")
-        nc.vector.tensor_tensor(new0a[:], y0[0][:], old0a[:], MIN)
+        project(0, keep.tile([P, H], U32, name="x_codes0", tag="x_codes", align_bytes=64))
+        old = [keep.tile([P, S], F32, name="old%d" % b) for b in range(2)]
+        for b in range(2):
+            look_up(old[b][:], b, 0, S)
+        new0a = keep.tile([P, H], F32, name="new0a")
+        new1a = keep.tile([P, H], F32, name="new1a")
+        nc.vector.tensor_tensor(new0a[:], y0[0], old[0][:, :H], MIN)
+        nc.vector.tensor_tensor(new1a[:], y1[0], old[1][:, :H], MIN)
         put_back(0, 0, H, new0a[:])
-
-        project(1, keep.tile([P, H], U32, name="x_codes1", tag="t1", align_bytes=64))
-        old1 = keep.tile([P, S], F32, name="old1", tag="t2")
-        look_up(old1[:], 1, 0, S)
+        project(1, keep.tile([P, H], U32, name="x_codes1", tag="x_codes", align_bytes=64))
+        put_back(1, 0, H, new1a[:])
         new0b = keep.tile([P, H], F32, name="new0b")
-        new1 = keep.tile([P, S], F32, name="new1")
-        nc.vector.tensor_tensor(new0b[:], y0[1][:], old0b[:], MIN)
-        nc.vector.tensor_tensor(new1[:], y1[:], old1[:], MIN)
+        new1b = keep.tile([P, H], F32, name="new1b")
+        nc.vector.tensor_tensor(new0b[:], y0[1], old[0][:, H:], MIN)
+        nc.vector.tensor_tensor(new1b[:], y1[1], old[1][:, H:], MIN)
         put_back(0, H, S, new0b[:])
         nc.sync.dma_start(out[0:P, :], store[0][:])
-        put_back(1, 0, S, new1[:])
+        put_back(1, H, S, new1b[:])
         nc.sync.dma_start(out[P : 2 * P, :], store[1][:])

@@ -17,22 +17,19 @@ def tile_picked_idxput_min_e_kernel(tc, xT, mem, w1_words, w1_scales, offs, slot
         offs_t = keep.tile([P, S // 16], U16, name="offs_t")
         slot_t = keep.tile([P, S // 16], U16, name="slot_t")
         w_scales = keep.tile([P, N], U8, name="w_scales", align_bytes=64)
-        w_codes = keep.tile([P, N], U32, name="w_codes", align_bytes=64)
         nc.gpsimd.memset(w_scales[:].bitcast(I32), 0)
         for q in range(4):
             nc.gpsimd.dma_start(w_scales[32 * q : 32 * q + 4, :].bitcast(I32), w1_scales[0, 4 * q : 4 * q + 4, :].bitcast(I32))
 
         x_rows = xT.rearrange("(p j) t -> p j t", j=4)
-        raw = [keep.tile([P, T], F32, name="raw%d" % j) for j in range(4)]
+        raw = [keep.tile([P, T], F32, name="raw%d" % j, align_bytes=64) for j in range(4)]
         store = [keep.tile([P, U], F32, name="store%d" % b) for b in range(2)]
-        for j in range(4):
-            nc.sync.dma_start(raw[j][:], x_rows[:, j, :])
-            if j == 0:
-                nc.sync.dma_start(offs_t[:], offs)
+        nc.sync.dma_start(offs_t[:], offs)
         nc.sync.dma_start(slot_t[:], slot)
-        nc.sync.dma_start(store[0][:], mem[0:P, :])
-        nc.sync.dma_start(store[1][:], mem[P : 2 * P, :])
-        nc.sync.dma_start(w_codes[:].bitcast(I32), w1_words[0].rearrange("p n t -> p (n t)").bitcast(I32))
+        for j in range(4):
+            nc.scalar.dma_start(raw[j][:], x_rows[:, j, :])
+        for b in range(2):
+            nc.scalar.dma_start(store[b][:], mem[b * P : (b + 1) * P, :])
 
         woven = [keep.tile([P, H, 4], BF16, name="woven%d" % h, align_bytes=64) for h in range(2)]
         for j in range(4):
@@ -40,6 +37,9 @@ def tile_picked_idxput_min_e_kernel(tc, xT, mem, w1_words, w1_scales, offs, slot
                 nc.vector.tensor_copy(woven[0][:, s0:s1, j], raw[j][:].indirect(offs_t[:, s0 // 16 : s1 // 16]))
             rounded = keep.tile([P, T], BF16, name="rounded%d" % j)
             nc.scalar.copy(rounded[:], raw[j][:])
+            if j == 1:
+                w_codes = keep.tile([P, N], U32, name="w_codes", tag="raw1", align_bytes=64)
+                nc.scalar.dma_start(w_codes[:].bitcast(I32), w1_words[0].rearrange("p n t -> p (n t)").bitcast(I32))
             nc.scalar.activation(woven[1][:, :, j], rounded[:].indirect(offs_t[:, H // 16 :]), COPY)
 
         ya = [psum.tile([P, H], F32, name="ya%d" % b) for b in range(2)]

@@ -16,10 +16,6 @@ def tile_picked_idxput_min_e_kernel(tc, xT, mem, w1_words, w1_scales, offs, slot
     with tc.tile_pool(name="keep", bufs=1) as keep, tc.psum_pool(name="psum", bufs=1) as psum:
         offs_t = keep.tile([P, S // 16], U16, name="offs_t")
         slot_t = keep.tile([P, S // 16], U16, name="slot_t")
-        w_scales = keep.tile([P, N], U8, name="w_scales", align_bytes=64)
-        nc.gpsimd.memset(w_scales[:].bitcast(I32), 0)
-        for q in range(4):
-            nc.gpsimd.dma_start(w_scales[32 * q : 32 * q + 4, :].bitcast(I32), w1_scales[0, 4 * q : 4 * q + 4, :].bitcast(I32))
 
         x_rows = xT.rearrange("(p j) t -> p j t", j=4)
         raw = [keep.tile([P, T], F32, name="raw%d" % j, align_bytes=64) for j in range(4)]
@@ -41,6 +37,11 @@ def tile_picked_idxput_min_e_kernel(tc, xT, mem, w1_words, w1_scales, offs, slot
                 w_codes = keep.tile([P, N], U32, name="w_codes", tag="raw1", align_bytes=64)
                 nc.scalar.dma_start(w_codes[:].bitcast(I32), w1_words[0].rearrange("p n t -> p (n t)").bitcast(I32))
             nc.scalar.activation(woven[1][:, :, j], rounded[:].indirect(offs_t[:, H // 16 :]), COPY)
+
+        w_scales = keep.tile([P, N], U8, name="w_scales", tag="raw0", align_bytes=64)
+        nc.gpsimd.memset(w_scales[:].bitcast(I32), 0)
+        for q in range(4):
+            nc.sync.dma_start(w_scales[32 * q : 32 * q + 4, :].bitcast(I32), w1_scales[0, 4 * q : 4 * q + 4, :].bitcast(I32))
 
         ya = [psum.tile([P, H], F32, name="ya%d" % b) for b in range(2)]
         yb = psum.tile([P, 2, H], F32, name="yb")

@@ -24,19 +24,24 @@ def tile_picked_idxput_min_e_kernel(tc, xT, mem, w1_words, w1_scales, offs, slot
         nc.sync.dma_start(slot_t[:], slot)
         for j in range(4):
             nc.scalar.dma_start(raw[j][:], x_rows[:, j, :])
-        for b in range(2):
-            nc.scalar.dma_start(store[b][:], mem[b * P : (b + 1) * P, :])
+            if j == 1:
+                nc.scalar.dma_start(store[0][:], mem[:P, :])
+        nc.scalar.dma_start(store[1][:], mem[P:, :])
+        old = [keep.tile([P, S], F32, name="old%d" % b) for b in range(2)]
 
-        woven = [keep.tile([P, H, 4], BF16, name="woven%d" % h, align_bytes=64) for h in range(2)]
+        whole = keep.tile([P, S, 4], BF16, name="whole", align_bytes=64)
+        woven = [whole[:, :H, :], whole[:, H:, :]]
         for j in range(4):
-            for s0, s1 in ((0, H),) if j < 3 else ((0, H // 2), (H // 2, H)):
-                nc.vector.tensor_copy(woven[0][:, s0:s1, j], raw[j][:].indirect(offs_t[:, s0 // 16 : s1 // 16]))
+            cut = H
+            for s0, s1 in ((0, cut),) if j < 3 else ((0, H // 2), (H // 2, H)):
+                nc.vector.tensor_copy(whole[:, s0:s1, j], raw[j][:].indirect(offs_t[:, s0 // 16 : s1 // 16]))
             rounded = keep.tile([P, T], BF16, name="rounded%d" % j)
             nc.scalar.copy(rounded[:], raw[j][:])
             if j == 1:
+                nc.vector.tensor_copy(old[0][:], store[0][:].indirect(slot_t[:]))
                 w_codes = keep.tile([P, N], U32, name="w_codes", tag="raw1", align_bytes=64)
                 nc.scalar.dma_start(w_codes[:].bitcast(I32), w1_words[0].rearrange("p n t -> p (n t)").bitcast(I32))
-            nc.scalar.activation(woven[1][:, :, j], rounded[:].indirect(offs_t[:, H // 16 :]), COPY)
+            nc.scalar.activation(whole[:, cut:, j], rounded[:].indirect(offs_t[:, cut // 16 :]), COPY)
 
         w_scales = keep.tile([P, N], U8, name="w_scales", tag="raw0", align_bytes=64)
         nc.gpsimd.memset(w_scales[:].bitcast(I32), 0)
@@ -73,9 +78,7 @@ def tile_picked_idxput_min_e_kernel(tc, xT, mem, w1_words, w1_scales, offs, slot
             nc.vector.tensor_copy(store[b][:].indirect(slot_t[:, s0 // 16 : s1 // 16]), src)
 
         project(0, keep.tile([P, H], U32, name="x_codes0", tag="x_codes", align_bytes=64))
-        old = [keep.tile([P, S], F32, name="old%d" % b) for b in range(2)]
-        for b in range(2):
-            look_up(old[b][:], b, 0, S)
+        look_up(old[1][:], 1, 0, S)
         new0a = keep.tile([P, H], F32, name="new0a")
         new1a = keep.tile([P, H], F32, name="new1a")
         nc.vector.tensor_tensor(new0a[:], y0[0], old[0][:, :H], MIN)

@@ -6,9 +6,11 @@ F32, BF16 = mybir.dt.float32, mybir.dt.bfloat16
 U32, I32, U16, U8 = mybir.dt.uint32, mybir.dt.int32, mybir.dt.uint16, mybir.dt.uint8
 FP8X4 = mybir.dt.float8_e4m3fn_x4
 COPY = mybir.ActivationFunctionType.Copy
-MIN = mybir.AluOpType.min
+MIN, MULT, ADD = mybir.AluOpType.min, mybir.AluOpType.mult, mybir.AluOpType.add
 FLOPS = 2 * K * S * N
 H = S // 2
+CUT = 320
+ORDER = (2, 0, 1, 3)
 
 
 def tile_picked_idxput_min_e_kernel(tc, xT, mem, w1_words, w1_scales, offs, slot, out):
@@ -16,53 +18,66 @@ def tile_picked_idxput_min_e_kernel(tc, xT, mem, w1_words, w1_scales, offs, slot
     with tc.tile_pool(name="keep", bufs=1) as keep, tc.psum_pool(name="psum", bufs=1) as psum:
         offs_t = keep.tile([P, S // 16], U16, name="offs_t")
         slot_t = keep.tile([P, S // 16], U16, name="slot_t")
-
         x_rows = xT.rearrange("(p j) t -> p j t", j=4)
         raw = [keep.tile([P, T], F32, name="raw%d" % j, align_bytes=64) for j in range(4)]
         store = [keep.tile([P, U], F32, name="store%d" % b) for b in range(2)]
         nc.sync.dma_start(offs_t[:], offs)
         nc.sync.dma_start(slot_t[:], slot)
-        for j in range(4):
+        for j in ORDER:
             nc.scalar.dma_start(raw[j][:], x_rows[:, j, :])
-            if j == 1:
-                nc.scalar.dma_start(store[0][:], mem[:P, :])
-        nc.scalar.dma_start(store[1][:], mem[P:, :])
+        for b in range(2):
+            nc.scalar.dma_start(store[b][:], mem[b * P : (b + 1) * P, :])
         old = [keep.tile([P, S], F32, name="old%d" % b) for b in range(2)]
 
-        whole = keep.tile([P, S, 4], BF16, name="whole", align_bytes=64)
-        woven = [whole[:, :H, :], whole[:, H:, :]]
-        for j in range(4):
-            cut = H
-            for s0, s1 in ((0, cut),) if j < 3 else ((0, H // 2), (H // 2, H)):
-                nc.vector.tensor_copy(whole[:, s0:s1, j], raw[j][:].indirect(offs_t[:, s0 // 16 : s1 // 16]))
-            rounded = keep.tile([P, T], BF16, name="rounded%d" % j)
-            nc.scalar.copy(rounded[:], raw[j][:])
-            if j == 1:
-                nc.vector.tensor_copy(old[0][:], store[0][:].indirect(slot_t[:]))
-                w_codes = keep.tile([P, N], U32, name="w_codes", tag="raw1", align_bytes=64)
-                nc.scalar.dma_start(w_codes[:].bitcast(I32), w1_words[0].rearrange("p n t -> p (n t)").bitcast(I32))
-            nc.scalar.activation(whole[:, cut:, j], rounded[:].indirect(offs_t[:, cut // 16 :]), COPY)
+        def picks(lst, s0, s1):
+            return lst[:, s0 // 16 : s1 // 16]
 
-        w_scales = keep.tile([P, N], U8, name="w_scales", tag="raw0", align_bytes=64)
+        whole = keep.tile([P, S, 4], BF16, name="whole", align_bytes=64)
+        rounded = [keep.tile([P, T], BF16, name="rounded%d" % j) for j in range(4)]
+        cut = (CUT, CUT, H, H)
+
+        def early(j, s0, s1):
+            nc.vector.tensor_copy(whole[:, s0:s1, j], raw[j][:].indirect(picks(offs_t, s0, s1)))
+
+        def late(j):
+            nc.scalar.activation(whole[:, cut[j] :, j], rounded[j][:].indirect(picks(offs_t, cut[j], S)), COPY)
+
+        for j in (2, 0, 1):
+            early(j, 0, cut[j])
+        early(3, 0, H // 2)
+        early(3, H // 2, H)
+        nc.gpsimd.tensor_scalar(rounded[1][:], raw[1][:], 1.0, 0.0, MULT, ADD)
+        nc.scalar.copy(rounded[2][:], raw[2][:])
+        nc.scalar.copy(rounded[0][:], raw[0][:])
+        w_codes = keep.tile([P, N], U32, name="w_codes", tag="raw0", align_bytes=64)
+        nc.scalar.dma_start(w_codes[:].bitcast(I32), w1_words[0].rearrange("p n t -> p (n t)").bitcast(I32))
+        late(2)
+        late(0)
+        nc.scalar.copy(rounded[3][:], raw[3][:])
+        late(1)
+        late(3)
+
+        w_scales = keep.tile([P, N], U8, name="w_scales", tag="raw2", align_bytes=64)
         nc.gpsimd.memset(w_scales[:].bitcast(I32), 0)
         for q in range(4):
             nc.sync.dma_start(w_scales[32 * q : 32 * q + 4, :].bitcast(I32), w1_scales[0, 4 * q : 4 * q + 4, :].bitcast(I32))
 
-        ya = [psum.tile([P, H], F32, name="ya%d" % b) for b in range(2)]
-        yb = psum.tile([P, 2, H], F32, name="yb")
-        y0 = [ya[0][:], yb[:, 0, :]]
-        y1 = [ya[1][:], yb[:, 1, :]]
+        y = [[psum.tile([P, H], F32, name="y%d_%d" % (b, h)) for h in range(2)] for b in range(2)]
+        new = [keep.tile([P, S], F32, name="new%d" % b) for b in range(2)]
 
-        def project(h, codes):
+        def project(h, pieces):
+            codes = keep.tile([P, H], U32, name="x_codes%d" % h, align_bytes=64)
             scales = keep.tile([P, H], U8, name="x_scales%d" % h, align_bytes=64)
-            for s0, s1 in ((0, H // 2), (H // 2, H)) if h == 0 else ((0, H),):
+            for s0, s1 in pieces:
                 nc.vector.quantize_mx(
-                    out=codes[:, s0:s1].bitcast(FP8X4), scales=scales[:, s0:s1], in_=woven[h][:, s0:s1, :].rearrange("p s j -> p (s j)")
+                    out=codes[:, s0:s1].bitcast(FP8X4),
+                    scales=scales[:, s0:s1],
+                    in_=whole[:, h * H + s0 : h * H + s1, :].rearrange("p s j -> p (s j)"),
                 )
-            for b, y in enumerate((y0[h], y1[h])):
+            for b in range(2):
                 cols = slice(b * P, (b + 1) * P)
                 nc.tensor.matmul_mx(
-                    out=y,
+                    out=y[b][h][:],
                     lhsT=w_codes[:, cols].bitcast(FP8X4),
                     lhsT_scale=w_scales[:, cols],
                     rhs=codes[:].bitcast(FP8X4),
@@ -71,26 +86,14 @@ def tile_picked_idxput_min_e_kernel(tc, xT, mem, w1_words, w1_scales, offs, slot
                     stop=True,
                 )
 
-        def look_up(dst, b, s0, s1):
-            nc.vector.tensor_copy(dst, store[b][:].indirect(slot_t[:, s0 // 16 : s1 // 16]))
-
-        def put_back(b, s0, s1, src):
-            nc.vector.tensor_copy(store[b][:].indirect(slot_t[:, s0 // 16 : s1 // 16]), src)
-
-        project(0, keep.tile([P, H], U32, name="x_codes0", tag="x_codes", align_bytes=64))
-        look_up(old[1][:], 1, 0, S)
-        new0a = keep.tile([P, H], F32, name="new0a")
-        new1a = keep.tile([P, H], F32, name="new1a")
-        nc.vector.tensor_tensor(new0a[:], y0[0], old[0][:, :H], MIN)
-        nc.vector.tensor_tensor(new1a[:], y1[0], old[1][:, :H], MIN)
-        put_back(0, 0, H, new0a[:])
-        project(1, keep.tile([P, H], U32, name="x_codes1", tag="x_codes", align_bytes=64))
-        put_back(1, 0, H, new1a[:])
-        new0b = keep.tile([P, H], F32, name="new0b")
-        new1b = keep.tile([P, H], F32, name="new1b")
-        nc.vector.tensor_tensor(new0b[:], y0[1], old[0][:, H:], MIN)
-        nc.vector.tensor_tensor(new1b[:], y1[1], old[1][:, H:], MIN)
-        put_back(0, H, S, new0b[:])
-        nc.sync.dma_start(out[0:P, :], store[0][:])
-        put_back(1, H, S, new1b[:])
-        nc.sync.dma_start(out[P : 2 * P, :], store[1][:])
+        project(0, ((0, H // 2), (H // 2, H)))
+        for b in range(2):
+            nc.vector.tensor_copy(old[b][:], store[b][:].indirect(slot_t[:]))
+        project(1, ((0, H),))
+        for h in range(2):
+            for b in range(2):
+                cols = slice(h * H, (h + 1) * H)
+                nc.vector.tensor_tensor(new[b][:, cols], y[b][h][:], old[b][:, cols], MIN)
+        for b in range(2):
+            nc.vector.tensor_copy(store[b][:].indirect(slot_t[:]), new[b][:])
+            nc.sync.dma_start(out[b * P : (b + 1) * P, :], store[b][:])

@@ -57,7 +57,7 @@ def tile_picked_idxput_min_e_kernel(tc, xT, mem, w1_words, w1_scales, offs, slot
         late(1)
         late(3)
 
-        w_scales = keep.tile([P, N], U8, name="w_scales", tag="raw2", align_bytes=64)
+        w_scales = keep.tile([P, N], U8, name="w_scales", tag="raw1", align_bytes=64)
         nc.gpsimd.memset(w_scales[:].bitcast(I32), 0)
         for q in range(4):
             nc.sync.dma_start(w_scales[32 * q : 32 * q + 4, :].bitcast(I32), w1_scales[0, 4 * q : 4 * q + 4, :].bitcast(I32))
@@ -90,10 +90,19 @@ def tile_picked_idxput_min_e_kernel(tc, xT, mem, w1_words, w1_scales, offs, slot
         for b in range(2):
             nc.vector.tensor_copy(old[b][:], store[b][:].indirect(slot_t[:]))
         project(1, ((0, H),))
-        for h in range(2):
-            for b in range(2):
-                cols = slice(h * H, (h + 1) * H)
-                nc.vector.tensor_tensor(new[b][:, cols], y[b][h][:], old[b][:, cols], MIN)
-        for b in range(2):
-            nc.vector.tensor_copy(store[b][:].indirect(slot_t[:]), new[b][:])
-            nc.sync.dma_start(out[b * P : (b + 1) * P, :], store[b][:])
+        def smaller(b, h):
+            cols = slice(h * H, (h + 1) * H)
+            nc.vector.tensor_tensor(new[b][:, cols], y[b][h][:], old[b][:, cols], MIN)
+
+        def put_back(b, s0, s1):
+            nc.vector.tensor_copy(store[b][:].indirect(picks(slot_t, s0, s1)), new[b][:, s0:s1])
+
+        smaller(0, 0)
+        smaller(1, 0)
+        put_back(0, 0, H)
+        smaller(0, 1)
+        smaller(1, 1)
+        put_back(0, H, S)
+        nc.sync.dma_start(out[:P, :], store[0][:])
+        put_back(1, 0, S)
+        nc.sync.dma_start(out[P:, :], store[1][:])

@@ -33,7 +33,7 @@ def tile_picked_idxput_min_e_kernel(tc, xT, mem, w1_words, w1_scales, offs, slot
             return lst[:, s0 // 16 : s1 // 16]
 
         whole = keep.tile([P, S, 4], BF16, name="whole", align_bytes=64)
-        rounded = [keep.tile([P, T], BF16, name="rounded%d" % j) for j in range(4)]
+        rounded = [keep.tile([P, T], BF16, name="rounded%d" % j, align_bytes=64) for j in range(4)]
         cut = (CUT, CUT, H, H)
 
         def early(j, s0, s1):
@@ -57,7 +57,7 @@ def tile_picked_idxput_min_e_kernel(tc, xT, mem, w1_words, w1_scales, offs, slot
         late(1)
         late(3)
 
-        w_scales = keep.tile([P, N], U8, name="w_scales", tag="raw1", align_bytes=64)
+        w_scales = keep.tile([P, N], U8, name="w_scales", tag="rounded0", align_bytes=64)
         nc.gpsimd.memset(w_scales[:].bitcast(I32), 0)
         for q in range(4):
             nc.sync.dma_start(w_scales[32 * q : 32 * q + 4, :].bitcast(I32), w1_scales[0, 4 * q : 4 * q + 4, :].bitcast(I32))

@@ -49,12 +49,14 @@ def tile_picked_idxput_min_e_kernel(tc, xT, mem, w1_words, w1_scales, offs, slot
         nc.gpsimd.tensor_scalar(rounded[1][:], raw[1][:], 1.0, 0.0, MULT, ADD)
         nc.scalar.copy(rounded[2][:], raw[2][:])
         nc.scalar.copy(rounded[0][:], raw[0][:])
-        w_codes = keep.tile([P, N], U32, name="w_codes", tag="raw0", align_bytes=64)
-        nc.scalar.dma_start(w_codes[:].bitcast(I32), w1_words[0].rearrange("p n t -> p (n t)").bitcast(I32))
+        w_words = w1_words[0].rearrange("p n t -> p (n t)").bitcast(I32)
+        w_codes = [keep.tile([P, P], U32, name="w_codes%d" % b, tag="raw%d" % (3 * b), align_bytes=64) for b in range(2)]
+        nc.scalar.dma_start(w_codes[0][:].bitcast(I32), w_words[:, :P])
         late(2)
         late(0)
         nc.scalar.copy(rounded[3][:], raw[3][:])
         late(1)
+        nc.scalar.dma_start(w_codes[1][:].bitcast(I32), w_words[:, P:])
         late(3)
 
         w_scales = keep.tile([P, N], U8, name="w_scales", tag="rounded0", align_bytes=64)
@@ -78,7 +80,7 @@ def tile_picked_idxput_min_e_kernel(tc, xT, mem, w1_words, w1_scales, offs, slot
                 cols = slice(b * P, (b + 1) * P)
                 nc.tensor.matmul_mx(
                     out=y[b][h][:],
-                    lhsT=w_codes[:, cols].bitcast(FP8X4),
+                    lhsT=w_codes[b][:].bitcast(FP8X4),
                     lhsT_scale=w_scales[:, cols],
                     rhs=codes[:].bitcast(FP8X4),
                     rhs_scale=scales[:],

@@ -6,7 +6,9 @@ F32, BF16 = mybir.dt.float32, mybir.dt.bfloat16
 U32, I32, U16, U8 = mybir.dt.uint32, mybir.dt.int32, mybir.dt.uint16, mybir.dt.uint8
 FP8X4 = mybir.dt.float8_e4m3fn_x4
 COPY = mybir.ActivationFunctionType.Copy
-MIN, MULT, ADD = mybir.AluOpType.min, mybir.AluOpType.mult, mybir.AluOpType.add
+SIGN = mybir.ActivationFunctionType.Sign
+MIN, MAX, MULT, ADD, SUB = (mybir.AluOpType.min, mybir.AluOpType.max, mybir.AluOpType.mult, mybir.AluOpType.add, mybir.AluOpType.subtract)
+LARGEST = 3.4028234663852886e38
 FLOPS = 2 * K * S * N
 H = S // 2
 CUT = 320
@@ -25,7 +27,7 @@ def tile_picked_idxput_min_e_kernel(tc, xT, mem, w1_words, w1_scales, offs, slot
         nc.sync.dma_start(slot_t[:], slot)
         for j in ORDER:
             nc.scalar.dma_start(raw[j][:], x_rows[:, j, :])
-        for b in range(2):
+        for b in (1, 0):
             nc.scalar.dma_start(store[b][:], mem[b * P : (b + 1) * P, :])
         old = [keep.tile([P, S], F32, name="old%d" % b) for b in range(2)]
 
@@ -67,7 +69,7 @@ def tile_picked_idxput_min_e_kernel(tc, xT, mem, w1_words, w1_scales, offs, slot
         y = [[psum.tile([P, H], F32, name="y%d_%d" % (b, h)) for h in range(2)] for b in range(2)]
         new = [keep.tile([P, S], F32, name="new%d" % b) for b in range(2)]
 
-        def project(h, pieces):
+        def project(h, pieces, blocks):
             codes = keep.tile([P, H], U32, name="x_codes%d" % h, align_bytes=64)
             scales = keep.tile([P, H], U8, name="x_scales%d" % h, align_bytes=64)
             for s0, s1 in pieces:
@@ -76,7 +78,7 @@ def tile_picked_idxput_min_e_kernel(tc, xT, mem, w1_words, w1_scales, offs, slot
                     scales=scales[:, s0:s1],
                     in_=whole[:, h * H + s0 : h * H + s1, :].rearrange("p s j -> p (s j)"),
                 )
-            for b in range(2):
+            for b in blocks:
                 cols = slice(b * P, (b + 1) * P)
                 nc.tensor.matmul_mx(
                     out=y[b][h][:],
@@ -88,10 +90,26 @@ def tile_picked_idxput_min_e_kernel(tc, xT, mem, w1_words, w1_scales, offs, slot
                     stop=True,
                 )
 
-        project(0, ((0, H // 2), (H // 2, H)))
-        for b in range(2):
+        project(0, ((0, H // 2), (H // 2, H)), (0, 1))
+        for b in (1, 0):
             nc.vector.tensor_copy(old[b][:], store[b][:].indirect(slot_t[:]))
-        project(1, ((0, H),))
+        capped = keep.tile([P, 2, H], F32, name="capped", tag="rounded1", align_bytes=64)
+        nc.gpsimd.tensor_scalar(capped[:, 0, :], old[1][:, H:], LARGEST, float("-inf"), MIN, MAX)
+        project(1, ((0, H),), (1, 0))
+
+        y_late = keep.tile([P, H], F32, name="y_late")
+        gap = keep.tile([P, H], F32, name="gap")
+        side = keep.tile([P, H], F32, name="side")
+        share = keep.tile([P, 2, H], F32, name="share")
+        terms = keep.tile([P, 2, H], F32, name="terms")
+        nc.scalar.copy(y_late[:], y[1][1][:])
+        nc.gpsimd.tensor_tensor(gap[:], capped[:, 0, :], y_late[:], SUB)
+        nc.gpsimd.tensor_scalar(capped[:, 1, :], y_late[:], LARGEST, float("-inf"), MIN, MAX)
+        nc.scalar.activation(side[:], gap[:], SIGN)
+        nc.scalar.activation(share[:, 0, :], side[:], COPY, scale=-0.5, bias=0.5)
+        nc.scalar.activation(share[:, 1, :], side[:], COPY, scale=0.5, bias=0.5)
+        nc.gpsimd.tensor_tensor(terms[:], capped[:], share[:], MULT)
+
         def smaller(b, h):
             cols = slice(h * H, (h + 1) * H)
             nc.vector.tensor_tensor(new[b][:, cols], y[b][h][:], old[b][:, cols], MIN)
@@ -103,8 +121,8 @@ def tile_picked_idxput_min_e_kernel(tc, xT, mem, w1_words, w1_scales, offs, slot
         smaller(1, 0)
         put_back(0, 0, H)
         smaller(0, 1)
-        smaller(1, 1)
+        put_back(1, 0, H)
         put_back(0, H, S)
         nc.sync.dma_start(out[:P, :], store[0][:])
-        put_back(1, 0, S)
+        nc.vector.tensor_tensor(store[1][:].indirect(picks(slot_t, H, S)), terms[:, 0, :], terms[:, 1, :], ADD)
         nc.sync.dma_start(out[P:, :], store[1][:])

@@ -29,7 +29,7 @@ def tile_picked_idxput_min_e_kernel(tc, xT, mem, w1_words, w1_scales, offs, slot
             nc.scalar.dma_start(raw[j][:], x_rows[:, j, :])
         for b in (1, 0):
             nc.scalar.dma_start(store[b][:], mem[b * P : (b + 1) * P, :])
-        old = [keep.tile([P, S], F32, name="old%d" % b) for b in range(2)]
+        old = [keep.tile([P, S + b * H], F32, name="old%d" % b) for b in range(2)]
 
         def picks(lst, s0, s1):
             return lst[:, s0 // 16 : s1 // 16]
@@ -51,14 +51,12 @@ def tile_picked_idxput_min_e_kernel(tc, xT, mem, w1_words, w1_scales, offs, slot
         nc.gpsimd.tensor_scalar(rounded[1][:], raw[1][:], 1.0, 0.0, MULT, ADD)
         nc.scalar.copy(rounded[2][:], raw[2][:])
         nc.scalar.copy(rounded[0][:], raw[0][:])
-        w_words = w1_words[0].rearrange("p n t -> p (n t)").bitcast(I32)
-        w_codes = [keep.tile([P, P], U32, name="w_codes%d" % b, tag="raw%d" % (3 * b), align_bytes=64) for b in range(2)]
-        nc.scalar.dma_start(w_codes[0][:].bitcast(I32), w_words[:, :P])
+        w_codes = keep.tile([P, N], U32, name="w_codes", tag="raw0", align_bytes=64)
+        nc.scalar.dma_start(w_codes[:].bitcast(I32), w1_words[0].rearrange("p n t -> p (n t)").bitcast(I32))
         late(2)
         late(0)
         nc.scalar.copy(rounded[3][:], raw[3][:])
         late(1)
-        nc.scalar.dma_start(w_codes[1][:].bitcast(I32), w_words[:, P:])
         late(3)
 
         w_scales = keep.tile([P, N], U8, name="w_scales", tag="rounded0", align_bytes=64)
@@ -82,7 +80,7 @@ def tile_picked_idxput_min_e_kernel(tc, xT, mem, w1_words, w1_scales, offs, slot
                 cols = slice(b * P, (b + 1) * P)
                 nc.tensor.matmul_mx(
                     out=y[b][h][:],
-                    lhsT=w_codes[b][:].bitcast(FP8X4),
+                    lhsT=w_codes[:, cols].bitcast(FP8X4),
                     lhsT_scale=w_scales[:, cols],
                     rhs=codes[:].bitcast(FP8X4),
                     rhs_scale=scales[:],
@@ -91,20 +89,19 @@ def tile_picked_idxput_min_e_kernel(tc, xT, mem, w1_words, w1_scales, offs, slot
                 )
 
         project(0, ((0, H // 2), (H // 2, H)), (0, 1))
-        for b in (1, 0):
-            nc.vector.tensor_copy(old[b][:], store[b][:].indirect(slot_t[:]))
-        capped = keep.tile([P, 2, H], F32, name="capped", tag="rounded1", align_bytes=64)
-        nc.gpsimd.tensor_scalar(capped[:, 0, :], old[1][:, H:], LARGEST, float("-inf"), MIN, MAX)
+        nc.vector.tensor_copy(old[1][:, :S], store[1][:].indirect(slot_t[:]))
+        nc.vector.tensor_copy(old[0][:], store[0][:].indirect(slot_t[:]))
+        capped = keep.tile([P, 2, H], F32, name="capped")
         project(1, ((0, H),), (1, 0))
 
-        y_late = keep.tile([P, H], F32, name="y_late")
+        y_late = old[1][:, S:]
         gap = keep.tile([P, H], F32, name="gap")
         side = keep.tile([P, H], F32, name="side")
         share = keep.tile([P, 2, H], F32, name="share")
         terms = keep.tile([P, 2, H], F32, name="terms")
-        nc.scalar.copy(y_late[:], y[1][1][:])
-        nc.gpsimd.tensor_tensor(gap[:], capped[:, 0, :], y_late[:], SUB)
-        nc.gpsimd.tensor_scalar(capped[:, 1, :], y_late[:], LARGEST, float("-inf"), MIN, MAX)
+        nc.scalar.copy(y_late, y[1][1][:])
+        nc.gpsimd.tensor_tensor(gap[:], old[1][:, H:S], y_late, SUB)
+        nc.gpsimd.tensor_scalar(capped[:].rearrange("p a s -> p (a s)"), old[1][:, H:], LARGEST, float("-inf"), MIN, MAX)
         nc.scalar.activation(side[:], gap[:], SIGN)
         nc.scalar.activation(share[:, 0, :], side[:], COPY, scale=-0.5, bias=0.5)
         nc.scalar.activation(share[:, 1, :], side[:], COPY, scale=0.5, bias=0.5)

@@ -6,13 +6,13 @@ F32, BF16 = mybir.dt.float32, mybir.dt.bfloat16
 U32, I32, U16, U8 = mybir.dt.uint32, mybir.dt.int32, mybir.dt.uint16, mybir.dt.uint8
 FP8X4 = mybir.dt.float8_e4m3fn_x4
 COPY = mybir.ActivationFunctionType.Copy
-SIGN = mybir.ActivationFunctionType.Sign
-MIN, MAX, MULT, ADD, SUB = (mybir.AluOpType.min, mybir.AluOpType.max, mybir.AluOpType.mult, mybir.AluOpType.add, mybir.AluOpType.subtract)
-LARGEST = 3.4028234663852886e38
+MIN = mybir.AluOpType.min
 FLOPS = 2 * K * S * N
 H = S // 2
-CUT = 320
-ORDER = (2, 0, 1, 3)
+ROW = 4
+LOOK = 384
+CUT = (320, 320)
+OWN = 320
 
 
 def tile_picked_idxput_min_e_kernel(tc, xT, mem, w1_words, w1_scales, offs, slot, out):
@@ -22,104 +22,90 @@ def tile_picked_idxput_min_e_kernel(tc, xT, mem, w1_words, w1_scales, offs, slot
         slot_t = keep.tile([P, S // 16], U16, name="slot_t")
         x_rows = xT.rearrange("(p j) t -> p j t", j=4)
         raw = [keep.tile([P, T], F32, name="raw%d" % j, align_bytes=64) for j in range(4)]
-        store = [keep.tile([P, U], F32, name="store%d" % b) for b in range(2)]
+        first = keep.tile([P, U], F32, name="first")
+        w_codes = keep.tile([P, N], U32, name="w_codes", align_bytes=64)
         nc.sync.dma_start(offs_t[:], offs)
-        nc.sync.dma_start(slot_t[:], slot)
-        for j in ORDER:
+        for j in range(4):
             nc.scalar.dma_start(raw[j][:], x_rows[:, j, :])
-        for b in (1, 0):
-            nc.scalar.dma_start(store[b][:], mem[b * P : (b + 1) * P, :])
-        old = [keep.tile([P, S + b * H], F32, name="old%d" % b) for b in range(2)]
+        nc.sync.dma_start(slot_t[:], slot)
+        nc.scalar.dma_start(w_codes[:].bitcast(I32), w1_words[0].rearrange("p n t -> p (n t)").bitcast(I32))
+        nc.scalar.dma_start(first[:], mem[:P, :])
 
         def picks(lst, s0, s1):
             return lst[:, s0 // 16 : s1 // 16]
 
         whole = keep.tile([P, S, 4], BF16, name="whole", align_bytes=64)
-        rounded = [keep.tile([P, T], BF16, name="rounded%d" % j, align_bytes=64) for j in range(4)]
-        cut = (CUT, CUT, H, H)
+        flat = [keep.tile([P, 2, S - CUT[u]], BF16, name="flat%d" % u) for u in range(2)]
 
-        def early(j, s0, s1):
+        def stepped(j, s0, s1):
             nc.vector.tensor_copy(whole[:, s0:s1, j], raw[j][:].indirect(picks(offs_t, s0, s1)))
 
-        def late(j):
-            nc.scalar.activation(whole[:, cut[j] :, j], rounded[j][:].indirect(picks(offs_t, cut[j], S)), COPY)
+        def plain(j):
+            nc.scalar.activation(flat[j // 2][:, j % 2, :], raw[j][:].indirect(picks(offs_t, CUT[j // 2], S)), COPY)
 
-        for j in (2, 0, 1):
-            early(j, 0, cut[j])
-        early(3, 0, H // 2)
-        early(3, H // 2, H)
-        nc.gpsimd.tensor_scalar(rounded[1][:], raw[1][:], 1.0, 0.0, MULT, ADD)
-        nc.scalar.copy(rounded[2][:], raw[2][:])
-        nc.scalar.copy(rounded[0][:], raw[0][:])
-        w_codes = keep.tile([P, N], U32, name="w_codes", tag="raw0", align_bytes=64)
-        nc.scalar.dma_start(w_codes[:].bitcast(I32), w1_words[0].rearrange("p n t -> p (n t)").bitcast(I32))
-        late(2)
-        late(0)
-        nc.scalar.copy(rounded[3][:], raw[3][:])
-        late(1)
-        late(3)
-
-        w_scales = keep.tile([P, N], U8, name="w_scales", tag="rounded0", align_bytes=64)
-        nc.gpsimd.memset(w_scales[:].bitcast(I32), 0)
+        for j in range(2):
+            stepped(j, 0, CUT[0])
+            plain(j)
+        scales = keep.tile([P, S], U8, name="scales", tag="raw0", align_bytes=64)
         for q in range(4):
-            nc.sync.dma_start(w_scales[32 * q : 32 * q + 4, :].bitcast(I32), w1_scales[0, 4 * q : 4 * q + 4, :].bitcast(I32))
+            rows = slice(32 * q + ROW, 32 * q + ROW + 4)
+            nc.sync.dma_start(scales[rows, :N].bitcast(I32), w1_scales[0, 4 * q : 4 * q + 4, :].bitcast(I32))
+        second = keep.tile([P, U], F32, name="second", tag="raw1", align_bytes=64)
+        nc.scalar.dma_start(second[:], mem[P:, :])
+        nc.scalar.copy(whole[:, CUT[0] :, 0:2], flat[0][:].rearrange("p e s -> p s e"))
+        stepped(2, 0, CUT[1])
+        plain(2)
+        stepped(3, 0, H // 2)
+        stepped(3, H // 2, CUT[1])
+        plain(3)
+        nc.scalar.copy(whole[:, CUT[1] :, 2:4], flat[1][:].rearrange("p e s -> p s e"))
 
-        y = [[psum.tile([P, H], F32, name="y%d_%d" % (b, h)) for h in range(2)] for b in range(2)]
-        new = [keep.tile([P, S], F32, name="new%d" % b) for b in range(2)]
+        codes = keep.tile([P, S], U32, name="x_codes", align_bytes=64)
+        y_first = [psum.tile([P, H], F32, name="y_first%d" % h) for h in range(2)]
+        y_second = psum.tile([P, S], F32, name="y_second")
 
-        def project(h, pieces, blocks):
-            codes = keep.tile([P, H], U32, name="x_codes%d" % h, align_bytes=64)
-            scales = keep.tile([P, H], U8, name="x_scales%d" % h, align_bytes=64)
-            for s0, s1 in pieces:
-                nc.vector.quantize_mx(
-                    out=codes[:, s0:s1].bitcast(FP8X4),
-                    scales=scales[:, s0:s1],
-                    in_=whole[:, h * H + s0 : h * H + s1, :].rearrange("p s j -> p (s j)"),
-                )
-            for b in blocks:
-                cols = slice(b * P, (b + 1) * P)
-                nc.tensor.matmul_mx(
-                    out=y[b][h][:],
-                    lhsT=w_codes[:, cols].bitcast(FP8X4),
-                    lhsT_scale=w_scales[:, cols],
-                    rhs=codes[:].bitcast(FP8X4),
-                    rhs_scale=scales[:],
-                    start=True,
-                    stop=True,
-                )
+        def quantise(s0, s1):
+            nc.vector.quantize_mx(
+                out=codes[:, s0:s1].bitcast(FP8X4),
+                scales=scales[:, s0:s1],
+                in_=whole[:, s0:s1, :].rearrange("p s j -> p (s j)"),
+            )
 
-        project(0, ((0, H // 2), (H // 2, H)), (0, 1))
-        nc.vector.tensor_copy(old[1][:, :S], store[1][:].indirect(slot_t[:]))
-        nc.vector.tensor_copy(old[0][:], store[0][:].indirect(slot_t[:]))
-        capped = keep.tile([P, 2, H], F32, name="capped")
-        project(1, ((0, H),), (1, 0))
+        def product(y, b, s0, s1):
+            cols = slice(b * P, (b + 1) * P)
+            nc.tensor.matmul_mx(
+                out=y,
+                lhsT=w_codes[:, cols].bitcast(FP8X4),
+                lhsT_scale=scales[ROW:, cols],
+                rhs=codes[:, s0:s1].bitcast(FP8X4),
+                rhs_scale=scales[:, s0:s1],
+                start=True,
+                stop=True,
+            )
 
-        y_late = old[1][:, S:]
-        gap = keep.tile([P, H], F32, name="gap")
-        side = keep.tile([P, H], F32, name="side")
-        share = keep.tile([P, 2, H], F32, name="share")
-        terms = keep.tile([P, 2, H], F32, name="terms")
-        nc.scalar.copy(y_late, y[1][1][:])
-        nc.gpsimd.tensor_tensor(gap[:], old[1][:, H:S], y_late, SUB)
-        nc.gpsimd.tensor_scalar(capped[:].rearrange("p a s -> p (a s)"), old[1][:, H:], LARGEST, float("-inf"), MIN, MAX)
-        nc.scalar.activation(side[:], gap[:], SIGN)
-        nc.scalar.activation(share[:, 0, :], side[:], COPY, scale=-0.5, bias=0.5)
-        nc.scalar.activation(share[:, 1, :], side[:], COPY, scale=0.5, bias=0.5)
-        nc.gpsimd.tensor_tensor(terms[:], capped[:], share[:], MULT)
+        quantise(0, H // 2)
+        quantise(H // 2, H)
+        product(y_first[0][:], 0, 0, H)
+        quantise(H, S)
+        product(y_first[1][:], 0, H, S)
+        product(y_second[:], 1, 0, S)
 
-        def smaller(b, h):
-            cols = slice(h * H, (h + 1) * H)
-            nc.vector.tensor_tensor(new[b][:, cols], y[b][h][:], old[b][:, cols], MIN)
+        old = keep.tile([P, H + S], F32, name="old", tag="flat1")
+        new_first = keep.tile([P, S], F32, name="new_first")
+        new_second = keep.tile([P, S], F32, name="new_second")
+        halves = ((0, H), (H, S))
+        for s0, s1 in ((0, H), (H, LOOK)):
+            nc.scalar.activation(old[:, s0:s1], first[:].indirect(picks(slot_t, s0, s1)), COPY)
+        nc.scalar.activation(old[:, H + OWN :], second[:].indirect(picks(slot_t, OWN, S)), COPY)
+        nc.vector.tensor_copy(old[:, LOOK:S], first[:].indirect(picks(slot_t, LOOK, S)))
+        for h, (s0, s1) in enumerate(halves):
+            nc.vector.tensor_tensor(new_first[:, s0:s1], y_first[h][:], old[:, s0:s1], MIN)
+        for s0, s1 in halves:
+            nc.scalar.activation(first[:].indirect(picks(slot_t, s0, s1)), new_first[:, s0:s1], COPY)
+        nc.sync.dma_start(out[:P, :], first[:])
 
-        def put_back(b, s0, s1):
-            nc.vector.tensor_copy(store[b][:].indirect(picks(slot_t, s0, s1)), new[b][:, s0:s1])
-
-        smaller(0, 0)
-        smaller(1, 0)
-        put_back(0, 0, H)
-        smaller(0, 1)
-        put_back(1, 0, H)
-        put_back(0, H, S)
-        nc.sync.dma_start(out[:P, :], store[0][:])
-        nc.vector.tensor_tensor(store[1][:].indirect(picks(slot_t, H, S)), terms[:, 0, :], terms[:, 1, :], ADD)
-        nc.sync.dma_start(out[P:, :], store[1][:])
+        nc.vector.tensor_copy(old[:, H : H + OWN], second[:].indirect(picks(slot_t, 0, OWN)))
+        for s0, s1 in ((OWN, S), (0, OWN)):
+            nc.vector.tensor_tensor(new_second[:, s0:s1], y_second[:, s0:s1], old[:, H + s0 : H + s1], MIN)
+        nc.vector.tensor_copy(second[:].indirect(slot_t[:]), new_second[:])
+        nc.sync.dma_start(out[P:, :], second[:])

@@ -25,11 +25,18 @@ def tile_picked_idxput_min_e_kernel(tc, xT, mem, w1_words, w1_scales, offs, slot
         first = keep.tile([P, U], F32, name="first")
         w_codes = keep.tile([P, N], U32, name="w_codes", align_bytes=64)
         nc.sync.dma_start(offs_t[:], offs)
-        for j in range(4):
-            nc.scalar.dma_start(raw[j][:], x_rows[:, j, :])
+        nc.scalar.dma_start(raw[0][:], x_rows[:, 0, :])
+        scales = keep.tile([P, S], U8, name="scales", align_bytes=64)
+        for q in range(4):
+            rows = slice(32 * q + ROW, 32 * q + ROW + 4)
+            nc.sync.dma_start(scales[rows, :N].bitcast(I32), w1_scales[0, 4 * q : 4 * q + 4, :].bitcast(I32))
+        for j in range(1, 4):
+            nc.sync.dma_start(raw[j][:], x_rows[:, j, :])
         nc.sync.dma_start(slot_t[:], slot)
-        nc.scalar.dma_start(w_codes[:].bitcast(I32), w1_words[0].rearrange("p n t -> p (n t)").bitcast(I32))
-        nc.scalar.dma_start(first[:], mem[:P, :])
+        nc.sync.dma_start(w_codes[:].bitcast(I32), w1_words[0].rearrange("p n t -> p (n t)").bitcast(I32))
+        nc.sync.dma_start(first[:], mem[:P, :])
+        second = keep.tile([P, U], F32, name="second")
+        nc.sync.dma_start(second[:], mem[P:, :])
 
         def picks(lst, s0, s1):
             return lst[:, s0 // 16 : s1 // 16]
@@ -46,12 +53,6 @@ def tile_picked_idxput_min_e_kernel(tc, xT, mem, w1_words, w1_scales, offs, slot
         for j in range(2):
             stepped(j, 0, CUT[0])
             plain(j)
-        scales = keep.tile([P, S], U8, name="scales", tag="raw0", align_bytes=64)
-        for q in range(4):
-            rows = slice(32 * q + ROW, 32 * q + ROW + 4)
-            nc.sync.dma_start(scales[rows, :N].bitcast(I32), w1_scales[0, 4 * q : 4 * q + 4, :].bitcast(I32))
-        second = keep.tile([P, U], F32, name="second", tag="raw1", align_bytes=64)
-        nc.scalar.dma_start(second[:], mem[P:, :])
         nc.scalar.copy(whole[:, CUT[0] :, 0:2], flat[0][:].rearrange("p e s -> p s e"))
         stepped(2, 0, CUT[1])
         plain(2)
@@ -100,7 +101,7 @@ def tile_picked_idxput_min_e_kernel(tc, xT, mem, w1_words, w1_scales, offs, slot
         nc.vector.tensor_copy(old[:, LOOK:S], first[:].indirect(picks(slot_t, LOOK, S)))
         for h, (s0, s1) in enumerate(halves):
             nc.vector.tensor_tensor(new_first[:, s0:s1], y_first[h][:], old[:, s0:s1], MIN)
-        for s0, s1 in halves:
+        for s0, s1 in reversed(halves):
             nc.scalar.activation(first[:].indirect(picks(slot_t, s0, s1)), new_first[:, s0:s1], COPY)
         nc.sync.dma_start(out[:P, :], first[:])
 

@@ -11,8 +11,8 @@ FLOPS = 2 * K * S * N
 H = S // 2
 ROW = 4
 LOOK = 384
-CUT = (320, 320)
-OWN = 320
+CUT = (256, 320)
+OWN = 256
 
 
 def tile_picked_idxput_min_e_kernel(tc, xT, mem, w1_words, w1_scales, offs, slot, out):

@@ -9,10 +9,9 @@ COPY = mybir.ActivationFunctionType.Copy
 MIN = mybir.AluOpType.min
 FLOPS = 2 * K * S * N
 H = S // 2
-ROW = 4
 LOOK = 384
 CUT = (256, 320)
-OWN = 256
+OWN = 320
 
 
 def tile_picked_idxput_min_e_kernel(tc, xT, mem, w1_words, w1_scales, offs, slot, out):
@@ -24,18 +23,22 @@ def tile_picked_idxput_min_e_kernel(tc, xT, mem, w1_words, w1_scales, offs, slot
         raw = [keep.tile([P, T], F32, name="raw%d" % j, align_bytes=64) for j in range(4)]
         first = keep.tile([P, U], F32, name="first")
         w_codes = keep.tile([P, N], U32, name="w_codes", align_bytes=64)
-        nc.sync.dma_start(offs_t[:], offs)
-        nc.scalar.dma_start(raw[0][:], x_rows[:, 0, :])
         scales = keep.tile([P, S], U8, name="scales", align_bytes=64)
-        for q in range(4):
-            rows = slice(32 * q + ROW, 32 * q + ROW + 4)
-            nc.sync.dma_start(scales[rows, :N].bitcast(I32), w1_scales[0, 4 * q : 4 * q + 4, :].bitcast(I32))
+        w_scales = keep.tile([P, N], U8, name="w_scales", align_bytes=64)
+        second = keep.tile([P, U], F32, name="second")
+        idle = keep.tile([P, 2], F32, name="idle")
+        nc.gpsimd.memset(idle[:, :1], 0.0)
+        nc.scalar.activation(idle[:, 1:], idle[:, :1], COPY)
+        nc.gpsimd.memset(w_scales[:].bitcast(I32), 0)
+        nc.sync.dma_start(offs_t[:], offs)
+        nc.sync.dma_start(raw[0][:], x_rows[:, 0, :])
+        nc.sync.dma_start(slot_t[:], slot)
         for j in range(1, 4):
             nc.sync.dma_start(raw[j][:], x_rows[:, j, :])
-        nc.sync.dma_start(slot_t[:], slot)
         nc.sync.dma_start(w_codes[:].bitcast(I32), w1_words[0].rearrange("p n t -> p (n t)").bitcast(I32))
+        for q in range(4):
+            nc.sync.dma_start(w_scales[32 * q : 32 * q + 4, :].bitcast(I32), w1_scales[0, 4 * q : 4 * q + 4, :].bitcast(I32))
         nc.sync.dma_start(first[:], mem[:P, :])
-        second = keep.tile([P, U], F32, name="second")
         nc.sync.dma_start(second[:], mem[P:, :])
 
         def picks(lst, s0, s1):
@@ -77,7 +80,7 @@ def tile_picked_idxput_min_e_kernel(tc, xT, mem, w1_words, w1_scales, offs, slot
             nc.tensor.matmul_mx(
                 out=y,
                 lhsT=w_codes[:, cols].bitcast(FP8X4),
-                lhsT_scale=scales[ROW:, cols],
+                lhsT_scale=w_scales[:, cols],
                 rhs=codes[:, s0:s1].bitcast(FP8X4),
                 rhs_scale=scales[:, s0:s1],
                 start=True,
@@ -91,13 +94,13 @@ def tile_picked_idxput_min_e_kernel(tc, xT, mem, w1_words, w1_scales, offs, slot
         product(y_first[1][:], 0, H, S)
         product(y_second[:], 1, 0, S)
 
-        old = keep.tile([P, H + S], F32, name="old", tag="flat1")
+        old = keep.tile([P, 2 * S], F32, name="old")
         new_first = keep.tile([P, S], F32, name="new_first")
         new_second = keep.tile([P, S], F32, name="new_second")
         halves = ((0, H), (H, S))
         for s0, s1 in ((0, H), (H, LOOK)):
             nc.scalar.activation(old[:, s0:s1], first[:].indirect(picks(slot_t, s0, s1)), COPY)
-        nc.scalar.activation(old[:, H + OWN :], second[:].indirect(picks(slot_t, OWN, S)), COPY)
+        nc.scalar.activation(old[:, S + OWN :], second[:].indirect(picks(slot_t, OWN, S)), COPY)
         nc.vector.tensor_copy(old[:, LOOK:S], first[:].indirect(picks(slot_t, LOOK, S)))
         for h, (s0, s1) in enumerate(halves):
             nc.vector.tensor_tensor(new_first[:, s0:s1], y_first[h][:], old[:, s0:s1], MIN)
@@ -105,8 +108,8 @@ def tile_picked_idxput_min_e_kernel(tc, xT, mem, w1_words, w1_scales, offs, slot
             nc.scalar.activation(first[:].indirect(picks(slot_t, s0, s1)), new_first[:, s0:s1], COPY)
         nc.sync.dma_start(out[:P, :], first[:])
 
-        nc.vector.tensor_copy(old[:, H : H + OWN], second[:].indirect(picks(slot_t, 0, OWN)))
+        nc.vector.tensor_copy(old[:, S : S + OWN], second[:].indirect(picks(slot_t, 0, OWN)))
         for s0, s1 in ((OWN, S), (0, OWN)):
-            nc.vector.tensor_tensor(new_second[:, s0:s1], y_second[:, s0:s1], old[:, H + s0 : H + s1], MIN)
+            nc.vector.tensor_tensor(new_second[:, s0:s1], y_second[:, s0:s1], old[:, S + s0 : S + s1], MIN)
         nc.vector.tensor_copy(second[:].indirect(slot_t[:]), new_second[:])
         nc.sync.dma_start(out[P:, :], second[:])

@@ -11,7 +11,7 @@ FLOPS = 2 * K * S * N
 H = S // 2
 LOOK = 384
 CUT = (256, 320)
-OWN = 320
+OWN = 384
 
 
 def tile_picked_idxput_min_e_kernel(tc, xT, mem, w1_words, w1_scales, offs, slot, out):
@@ -106,7 +106,7 @@ def tile_picked_idxput_min_e_kernel(tc, xT, mem, w1_words, w1_scales, offs, slot
             nc.vector.tensor_tensor(new_first[:, s0:s1], y_first[h][:], old[:, s0:s1], MIN)
         for s0, s1 in reversed(halves):
             nc.scalar.activation(first[:].indirect(picks(slot_t, s0, s1)), new_first[:, s0:s1], COPY)
-        nc.sync.dma_start(out[:P, :], first[:])
+        nc.scalar.dma_start(out[:P, :], first[:])
 
         nc.vector.tensor_copy(old[:, S : S + OWN], second[:].indirect(picks(slot_t, 0, OWN)))
         for s0, s1 in ((OWN, S), (0, OWN)):

@@ -9,9 +9,11 @@ COPY = mybir.ActivationFunctionType.Copy
 MIN = mybir.AluOpType.min
 FLOPS = 2 * K * S * N
 H = S // 2
-LOOK = 384
-CUT = (256, 320)
-OWN = 384
+LEAD = 128
+LATE = 384
+OWN = 320
+JOIN = 64
+LINE = 256
 
 
 def tile_picked_idxput_min_e_kernel(tc, xT, mem, w1_words, w1_scales, offs, slot, out):
@@ -20,53 +22,51 @@ def tile_picked_idxput_min_e_kernel(tc, xT, mem, w1_words, w1_scales, offs, slot
         offs_t = keep.tile([P, S // 16], U16, name="offs_t")
         slot_t = keep.tile([P, S // 16], U16, name="slot_t")
         x_rows = xT.rearrange("(p j) t -> p j t", j=4)
-        raw = [keep.tile([P, T], F32, name="raw%d" % j, align_bytes=64) for j in range(4)]
-        first = keep.tile([P, U], F32, name="first")
-        w_codes = keep.tile([P, N], U32, name="w_codes", align_bytes=64)
-        scales = keep.tile([P, S], U8, name="scales", align_bytes=64)
+        raw = [keep.tile([P, T], F32, name="raw%d" % j, align_bytes=LINE) for j in range(4)]
+        first = keep.tile([P, U], F32, name="first", align_bytes=LINE)
+        second = keep.tile([P, U], F32, name="second", align_bytes=LINE)
+        w_codes = keep.tile([P, N], U32, name="w_codes", align_bytes=LINE)
+        staged = keep.tile([4, 4, N], U8, name="staged", align_bytes=LINE)
         w_scales = keep.tile([P, N], U8, name="w_scales", align_bytes=64)
-        second = keep.tile([P, U], F32, name="second")
+        scales = keep.tile([P, S], U8, name="scales", align_bytes=64)
         idle = keep.tile([P, 2], F32, name="idle")
         nc.gpsimd.memset(idle[:, :1], 0.0)
         nc.scalar.activation(idle[:, 1:], idle[:, :1], COPY)
         nc.gpsimd.memset(w_scales[:].bitcast(I32), 0)
         nc.sync.dma_start(offs_t[:], offs)
         nc.sync.dma_start(raw[0][:], x_rows[:, 0, :])
-        nc.sync.dma_start(slot_t[:], slot)
+        nc.sync.dma_start(staged[:].bitcast(I32), w1_scales[0].rearrange("(q r) c -> r q c", r=4).bitcast(I32))
         for j in range(1, 4):
             nc.sync.dma_start(raw[j][:], x_rows[:, j, :])
-        nc.sync.dma_start(w_codes[:].bitcast(I32), w1_words[0].rearrange("p n t -> p (n t)").bitcast(I32))
-        for q in range(4):
-            nc.sync.dma_start(w_scales[32 * q : 32 * q + 4, :].bitcast(I32), w1_scales[0, 4 * q : 4 * q + 4, :].bitcast(I32))
+        nc.sync.dma_start(slot_t[:], slot)
         nc.sync.dma_start(first[:], mem[:P, :])
+        nc.sync.dma_start(w_codes[:].bitcast(I32), w1_words[0].rearrange("p n t -> p (n t)").bitcast(I32))
         nc.sync.dma_start(second[:], mem[P:, :])
 
         def picks(lst, s0, s1):
             return lst[:, s0 // 16 : s1 // 16]
 
         whole = keep.tile([P, S, 4], BF16, name="whole", align_bytes=64)
-        flat = [keep.tile([P, 2, S - CUT[u]], BF16, name="flat%d" % u) for u in range(2)]
 
-        def stepped(j, s0, s1):
+        def pick_x(j, s0, s1):
             nc.vector.tensor_copy(whole[:, s0:s1, j], raw[j][:].indirect(picks(offs_t, s0, s1)))
 
-        def plain(j):
-            nc.scalar.activation(flat[j // 2][:, j % 2, :], raw[j][:].indirect(picks(offs_t, CUT[j // 2], S)), COPY)
-
-        for j in range(2):
-            stepped(j, 0, CUT[0])
-            plain(j)
-        nc.scalar.copy(whole[:, CUT[0] :, 0:2], flat[0][:].rearrange("p e s -> p s e"))
-        stepped(2, 0, CUT[1])
-        plain(2)
-        stepped(3, 0, H // 2)
-        stepped(3, H // 2, CUT[1])
-        plain(3)
-        nc.scalar.copy(whole[:, CUT[1] :, 2:4], flat[1][:].rearrange("p e s -> p s e"))
+        for j in range(4):
+            if j < 3:
+                pick_x(j, 0, H)
+            else:
+                pick_x(j, 0, LEAD)
+                pick_x(j, LEAD, H)
+            nc.scalar.activation(whole[:, H:, j], raw[j][:].indirect(picks(offs_t, H, S)), COPY)
+            if j == 0:
+                for q in range(4):
+                    nc.vector.tensor_copy(w_scales[32 * q : 32 * q + 4, :].bitcast(I32), staged[:, q, :].bitcast(I32))
 
         codes = keep.tile([P, S], U32, name="x_codes", align_bytes=64)
-        y_first = [psum.tile([P, H], F32, name="y_first%d" % h) for h in range(2)]
-        y_second = psum.tile([P, S], F32, name="y_second")
+        y_lead = psum.tile([P, LEAD], F32, name="y_lead")
+        y_body = psum.tile([P, LATE - LEAD], F32, name="y_body")
+        y_join = psum.tile([P, S - LATE + H], F32, name="y_join")
+        y_tail = psum.tile([P, H], F32, name="y_tail")
 
         def quantise(s0, s1):
             nc.vector.quantize_mx(
@@ -87,29 +87,34 @@ def tile_picked_idxput_min_e_kernel(tc, xT, mem, w1_words, w1_scales, offs, slot
                 stop=True,
             )
 
-        quantise(0, H // 2)
-        quantise(H // 2, H)
-        product(y_first[0][:], 0, 0, H)
+        quantise(0, LEAD)
+        quantise(LEAD, H)
         quantise(H, S)
-        product(y_first[1][:], 0, H, S)
-        product(y_second[:], 1, 0, S)
+        product(y_lead[:], 0, 0, LEAD)
+        product(y_body[:], 0, LEAD, LATE)
+        product(y_join[:, : S - LATE], 0, LATE, S)
+        product(y_join[:, S - LATE :], 1, 0, H)
+        product(y_tail[:], 1, H, S)
 
         old = keep.tile([P, 2 * S], F32, name="old")
-        new_first = keep.tile([P, S], F32, name="new_first")
-        new_second = keep.tile([P, S], F32, name="new_second")
-        halves = ((0, H), (H, S))
-        for s0, s1 in ((0, H), (H, LOOK)):
-            nc.scalar.activation(old[:, s0:s1], first[:].indirect(picks(slot_t, s0, s1)), COPY)
-        nc.scalar.activation(old[:, S + OWN :], second[:].indirect(picks(slot_t, OWN, S)), COPY)
-        nc.vector.tensor_copy(old[:, LOOK:S], first[:].indirect(picks(slot_t, LOOK, S)))
-        for h, (s0, s1) in enumerate(halves):
-            nc.vector.tensor_tensor(new_first[:, s0:s1], y_first[h][:], old[:, s0:s1], MIN)
-        for s0, s1 in reversed(halves):
-            nc.scalar.activation(first[:].indirect(picks(slot_t, s0, s1)), new_first[:, s0:s1], COPY)
-        nc.scalar.dma_start(out[:P, :], first[:])
+        new = keep.tile([P, 2 * S], F32, name="new")
 
-        nc.vector.tensor_copy(old[:, S : S + OWN], second[:].indirect(picks(slot_t, 0, OWN)))
-        for s0, s1 in ((OWN, S), (0, OWN)):
-            nc.vector.tensor_tensor(new_second[:, s0:s1], y_second[:, s0:s1], old[:, S + s0 : S + s1], MIN)
-        nc.vector.tensor_copy(second[:].indirect(slot_t[:]), new_second[:])
+        def least(y, c0, c1):
+            nc.vector.tensor_tensor(new[:, c0:c1], y, old[:, c0:c1], MIN)
+
+        for s0, s1 in ((0, LEAD), (LEAD, H), (LATE, S)):
+            nc.scalar.activation(old[:, s0:s1], first[:].indirect(picks(slot_t, s0, s1)), COPY)
+        nc.vector.tensor_copy(old[:, H:LATE], first[:].indirect(picks(slot_t, H, LATE)))
+        least(y_lead[:], 0, LEAD)
+        least(y_body[:], LEAD, LATE)
+        nc.scalar.activation(first[:].indirect(picks(slot_t, 0, LEAD)), new[:, :LEAD], COPY)
+        nc.scalar.activation(old[:, S + OWN :], second[:].indirect(picks(slot_t, OWN, S)), COPY)
+        for s0, s1 in ((0, JOIN), (JOIN, OWN)):
+            nc.vector.tensor_copy(old[:, S + s0 : S + s1], second[:].indirect(picks(slot_t, s0, s1)))
+        least(y_join[:, : S - LATE + JOIN], LATE, S + JOIN)
+        nc.scalar.activation(first[:].indirect(picks(slot_t, LEAD, S)), new[:, LEAD:S], COPY)
+        nc.scalar.dma_start(out[:P, :], first[:])
+        least(y_join[:, S - LATE + JOIN :], S + JOIN, S + H)
+        least(y_tail[:], S + H, 2 * S)
+        nc.vector.tensor_copy(second[:].indirect(slot_t[:]), new[:, S:])
         nc.sync.dma_start(out[P:, :], second[:])

@@ -11,7 +11,7 @@ FLOPS = 2 * K * S * N
 H = S // 2
 LEAD = 128
 LATE = 384
-OWN = 320
+OWN = 256
 JOIN = 64
 LINE = 256
 

@@ -11,7 +11,7 @@ FLOPS = 2 * K * S * N
 H = S // 2
 LEAD = 128
 LATE = 384
-OWN = 256
+OWN = 192
 JOIN = 64
 LINE = 256
 
@@ -108,7 +108,8 @@ def tile_picked_idxput_min_e_kernel(tc, xT, mem, w1_words, w1_scales, offs, slot
         least(y_lead[:], 0, LEAD)
         least(y_body[:], LEAD, LATE)
         nc.scalar.activation(first[:].indirect(picks(slot_t, 0, LEAD)), new[:, :LEAD], COPY)
-        nc.scalar.activation(old[:, S + OWN :], second[:].indirect(picks(slot_t, OWN, S)), COPY)
+        for s0, s1 in ((OWN, H), (H, S)):
+            nc.scalar.activation(old[:, S + s0 : S + s1], second[:].indirect(picks(slot_t, s0, s1)), COPY)
         for s0, s1 in ((0, JOIN), (JOIN, OWN)):
             nc.vector.tensor_copy(old[:, S + s0 : S + s1], second[:].indirect(picks(slot_t, s0, s1)))
         least(y_join[:, : S - LATE + JOIN], LATE, S + JOIN)

@@ -13,6 +13,7 @@ LEAD = 128
 LATE = 384
 OWN = 192
 JOIN = 64
+LAST = 192
 LINE = 256
 
 
@@ -52,12 +53,9 @@ def tile_picked_idxput_min_e_kernel(tc, xT, mem, w1_words, w1_scales, offs, slot
             nc.vector.tensor_copy(whole[:, s0:s1, j], raw[j][:].indirect(picks(offs_t, s0, s1)))
 
         for j in range(4):
-            if j < 3:
-                pick_x(j, 0, H)
-            else:
-                pick_x(j, 0, LEAD)
-                pick_x(j, LEAD, H)
-            nc.scalar.activation(whole[:, H:, j], raw[j][:].indirect(picks(offs_t, H, S)), COPY)
+            cut = H if j < 2 else LAST
+            pick_x(j, 0, cut)
+            nc.scalar.activation(whole[:, cut:, j], raw[j][:].indirect(picks(offs_t, cut, S)), COPY)
             if j == 0:
                 for q in range(4):
                     nc.vector.tensor_copy(w_scales[32 * q : 32 * q + 4, :].bitcast(I32), staged[:, q, :].bitcast(I32))
@@ -88,8 +86,7 @@ def tile_picked_idxput_min_e_kernel(tc, xT, mem, w1_words, w1_scales, offs, slot
             )
 
         quantise(0, LEAD)
-        quantise(LEAD, H)
-        quantise(H, S)
+        quantise(LEAD, S)
         product(y_lead[:], 0, 0, LEAD)
         product(y_body[:], 0, LEAD, LATE)
         product(y_join[:, : S - LATE], 0, LATE, S)

import concourse.mybir as mybir

K, T, S, N, U = 512, 1024, 512, 256, 1024
P = 128
F32, BF16 = mybir.dt.float32, mybir.dt.bfloat16
U32, I32, U16, U8 = mybir.dt.uint32, mybir.dt.int32, mybir.dt.uint16, mybir.dt.uint8
FP8X4 = mybir.dt.float8_e4m3fn_x4
COPY = mybir.ActivationFunctionType.Copy
MIN = mybir.AluOpType.min
FLOPS = 2 * K * S * N
H = S // 2
LEAD = 128
LATE = 384
OWN = 192
JOIN = 64
LAST = 192
LINE = 256


def tile_picked_idxput_min_e_kernel(tc, xT, mem, w1_words, w1_scales, offs, slot, out):
    nc = tc.nc
    with tc.tile_pool(name="keep", bufs=1) as keep, tc.psum_pool(name="psum", bufs=1) as psum:
        offs_t = keep.tile([P, S // 16], U16, name="offs_t")
        slot_t = keep.tile([P, S // 16], U16, name="slot_t")
        x_rows = xT.rearrange("(p j) t -> p j t", j=4)
        raw = [keep.tile([P, T], F32, name="raw%d" % j, align_bytes=LINE) for j in range(4)]
        first = keep.tile([P, U], F32, name="first", align_bytes=LINE)
        second = keep.tile([P, U], F32, name="second", align_bytes=LINE)
        w_codes = keep.tile([P, N], U32, name="w_codes", align_bytes=LINE)
        staged = keep.tile([4, 4, N], U8, name="staged", align_bytes=LINE)
        w_scales = keep.tile([P, N], U8, name="w_scales", align_bytes=64)
        scales = keep.tile([P, S], U8, name="scales", align_bytes=64)
        idle = keep.tile([P, 2], F32, name="idle")
        nc.gpsimd.memset(idle[:, :1], 0.0)
        nc.scalar.activation(idle[:, 1:], idle[:, :1], COPY)
        nc.gpsimd.memset(w_scales[:].bitcast(I32), 0)
        nc.sync.dma_start(offs_t[:], offs)
        nc.sync.dma_start(raw[0][:], x_rows[:, 0, :])
        nc.sync.dma_start(staged[:].bitcast(I32), w1_scales[0].rearrange("(q r) c -> r q c", r=4).bitcast(I32))
        for j in range(1, 4):
            nc.sync.dma_start(raw[j][:], x_rows[:, j, :])
        nc.sync.dma_start(slot_t[:], slot)
        nc.sync.dma_start(first[:], mem[:P, :])
        nc.sync.dma_start(w_codes[:].bitcast(I32), w1_words[0].rearrange("p n t -> p (n t)").bitcast(I32))
        nc.sync.dma_start(second[:], mem[P:, :])

        def picks(lst, s0, s1):
            return lst[:, s0 // 16 : s1 // 16]

        whole = keep.tile([P, S, 4], BF16, name="whole", align_bytes=64)

        def pick_x(j, s0, s1):
            nc.vector.tensor_copy(whole[:, s0:s1, j], raw[j][:].indirect(picks(offs_t, s0, s1)))

        for j in range(4):
            cut = H if j < 2 else LAST
            pick_x(j, 0, cut)
            nc.scalar.activation(whole[:, cut:, j], raw[j][:].indirect(picks(offs_t, cut, S)), COPY)
            if j == 0:
                for q in range(4):
                    nc.vector.tensor_copy(w_scales[32 * q : 32 * q + 4, :].bitcast(I32), staged[:, q, :].bitcast(I32))

        codes = keep.tile([P, S], U32, name="x_codes", align_bytes=64)
        y_lead = psum.tile([P, LEAD], F32, name="y_lead")
        y_body = psum.tile([P, LATE - LEAD], F32, name="y_body")
        y_join = psum.tile([P, S - LATE + H], F32, name="y_join")
        y_tail = psum.tile([P, H], F32, name="y_tail")

        def quantise(s0, s1):
            nc.vector.quantize_mx(
                out=codes[:, s0:s1].bitcast(FP8X4),
                scales=scales[:, s0:s1],
                in_=whole[:, s0:s1, :].rearrange("p s j -> p (s j)"),
            )

        def product(y, b, s0, s1):
            cols = slice(b * P, (b + 1) * P)
            nc.tensor.matmul_mx(
                out=y,
                lhsT=w_codes[:, cols].bitcast(FP8X4),
                lhsT_scale=w_scales[:, cols],
                rhs=codes[:, s0:s1].bitcast(FP8X4),
                rhs_scale=scales[:, s0:s1],
                start=True,
                stop=True,
            )

        quantise(0, LEAD)
        quantise(LEAD, S)
        product(y_lead[:], 0, 0, LEAD)
        product(y_body[:], 0, LEAD, LATE)
        product(y_join[:, : S - LATE], 0, LATE, S)
        product(y_join[:, S - LATE :], 1, 0, H)
        product(y_tail[:], 1, H, S)

        old = keep.tile([P, 2 * S], F32, name="old")
        new = keep.tile([P, 2 * S], F32, name="new")

        def least(y, c0, c1):
            nc.vector.tensor_tensor(new[:, c0:c1], y, old[:, c0:c1], MIN)

        for s0, s1 in ((0, LEAD), (LEAD, H), (LATE, S)):
            nc.scalar.activation(old[:, s0:s1], first[:].indirect(picks(slot_t, s0, s1)), COPY)
        nc.vector.tensor_copy(old[:, H:LATE], first[:].indirect(picks(slot_t, H, LATE)))
        least(y_lead[:], 0, LEAD)
        least(y_body[:], LEAD, LATE)
        nc.scalar.activation(first[:].indirect(picks(slot_t, 0, LEAD)), new[:, :LEAD], COPY)
        for s0, s1 in ((OWN, H), (H, S)):
            nc.scalar.activation(old[:, S + s0 : S + s1], second[:].indirect(picks(slot_t, s0, s1)), COPY)
        for s0, s1 in ((0, JOIN), (JOIN, OWN)):
            nc.vector.tensor_copy(old[:, S + s0 : S + s1], second[:].indirect(picks(slot_t, s0, s1)))
        least(y_join[:, : S - LATE + JOIN], LATE, S + JOIN)
        nc.scalar.activation(first[:].indirect(picks(slot_t, LEAD, S)), new[:, LEAD:S], COPY)
        nc.scalar.dma_start(out[:P, :], first[:])
        least(y_join[:, S - LATE + JOIN :], S + JOIN, S + H)
        least(y_tail[:], S + H, 2 * S)
        nc.vector.tensor_copy(second[:].indirect(slot_t[:]), new[:, S:])
        nc.sync.dma_start(out[P:, :], second[:])
